import numpy as np
import ml_dtypes


def mxq(x, axis, fmt="e4m3"):
    dtype, down = {"e4m3": (ml_dtypes.float8_e4m3fn, 7), "e5m2": (ml_dtypes.float8_e5m2, 14)}[fmt]
    v = np.moveaxis(np.asarray(x, np.float32).astype(ml_dtypes.bfloat16).astype(np.float64), axis, -1)
    blocks = v.reshape(v.shape[:-1] + (-1, 32))
    amax = np.abs(blocks).max(-1, keepdims=True)
    byte = np.maximum(np.where(amax > 0, np.frexp(amax)[1] - 1 + 127, 0) - down, 1)
    scale = np.exp2(byte - 127.0)
    codes = (blocks / scale).astype(np.float32).astype(dtype).astype(np.float64)
    return np.moveaxis((codes * scale).reshape(v.shape), -1, axis)


WIDE = False


def mx_kscale(k):
    if not WIDE:
        return np.ones(k)
    levels = np.array([10, -10, 5, -5, 0])
    if k % 512:
        return np.exp2(np.random.permutation(np.resize(levels, k // 32))).repeat(32)
    a = np.empty((k // 512, 16))
    for p in range(k // 512):
        a[p, :8] = np.random.permutation(np.resize(levels, 8))
        for g in range(8):
            far = levels[np.abs(levels - a[p, g]) >= 10]
            a[p, g + 8] = far[np.random.randint(len(far))]
    return np.exp2(a.ravel()).repeat(32)


def f64(x):
    return np.asarray(x).astype(np.float64)


def striped(idx):
    return np.tile(np.asarray(idx).reshape(-1, 16).T, (8, 1)).astype(np.uint16)


def unstriped(offs):
    return offs[:16].T.reshape(-1).astype(np.int64)


B, N, T, D, NQ = 1, 512, 2048, 512, 256


def setup_inputs():
    n = np.random.standard_normal
    idx = np.random.permutation(T)[:B * N]
    s = mx_kscale(D)[:, None]
    mid = n((D, T))
    return {
        "qT": (n((B, D, NQ)) * s * (1.00 / np.sqrt(D))).astype(np.float32),
        "kT": ((mid + np.abs(n((D, T)))) / s).astype(np.float32),
        "cT": ((mid - np.abs(n((D, T)))) / s).astype(np.float32),
        "offs": striped(idx),
    }


def reference(qT, kT, cT, offs):
    idx = unstriped(offs)
    pick = lambda x, which: x[:, which].reshape(x.shape[0], B, -1).transpose(1, 0, 2)
    kg = mxq(pick(f64(kT), idx), 1, "e4m3")
    cg = mxq(pick(f64(cT), idx), 1, "e4m3")
    hiq = mxq(np.maximum(f64(qT), 0.0), 1, "e4m3")
    loq = mxq(np.minimum(f64(qT), 0.0), 1, "e4m3")
    a = (hiq.transpose(0, 2, 1) @ kg) + (loq.transpose(0, 2, 1) @ cg)
    return a

@@ -1,0 +1,104 @@
+from contextlib import ExitStack
+
+import concourse.mybir as mybir
+
+D, T, N, NQ = 512, 2048, 512, 256
+FLOPS = 2 * 2 * NQ * D * N
+
+F32 = mybir.dt.float32
+BF16 = mybir.dt.bfloat16
+U32 = mybir.dt.uint32
+U16 = mybir.dt.uint16
+U8 = mybir.dt.uint8
+FP8X4 = mybir.dt.float8_e4m3fn_x4
+RELU = mybir.ActivationFunctionType.Relu
+
+P = 128
+PACK = 4
+HALF = N // 2
+
+
+def tile_attend_quest_f_topk_kernel(tc, qT, kT, cT, offs, out):
+    nc = tc.nc
+    with ExitStack() as ctx:
+        keep = ctx.enter_context(tc.tile_pool(name="keep", bufs=1))
+        psum = ctx.enter_context(tc.psum_pool(name="psum", bufs=1))
+
+        offsets = keep.tile([P, N // 16], U16, name="offsets")
+        q_raw = keep.tile([P, PACK, NQ], F32, name="q_raw")
+        k_planes = [keep.tile([P, T], F32, name="k_plane%d" % t) for t in range(PACK)]
+        c_planes = [keep.tile([P, T], F32, name="c_plane%d" % t) for t in range(PACK)]
+        k_rows = kT.rearrange("(p t) w -> p t w", t=PACK)
+        c_rows = cT.rearrange("(p t) w -> p t w", t=PACK)
+
+        nc.sync.dma_start(out=q_raw[:], in_=qT[0].rearrange("(p t) w -> p t w", t=PACK))
+        nc.sync.dma_start(offsets[:], offs)
+        for t in range(PACK):
+            nc.sync.dma_start(out=k_planes[t][:], in_=k_rows[:, t, :])
+        for t in range(PACK):
+            nc.sync.dma_start(out=c_planes[t][:], in_=c_rows[:, t, :])
+
+        def quantize(codes, scales, grouped, cols):
+            nc.vector.quantize_mx(
+                out=codes[:, cols].bitcast(FP8X4),
+                scales=scales[:, cols],
+                in_=grouped[:, cols, :].rearrange("p w t -> p (w t)"),
+            )
+
+        q_view = q_raw[:].rearrange("p t w -> p w t")
+        hi = keep.tile([P, NQ, PACK], BF16, name="hi", align_bytes=64)
+        lo = keep.tile([P, NQ, PACK], BF16, name="lo", align_bytes=64)
+        nc.scalar.activation(hi[:], q_view, RELU)
+        nc.vector.tensor_scalar_min(lo[:], q_view, 0.0)
+        hi_codes = keep.tile([P, NQ], U32, name="hi_codes", align_bytes=64)
+        hi_scales = keep.tile([P, NQ], U8, name="hi_scales", align_bytes=64)
+        lo_codes = keep.tile([P, NQ], U32, name="lo_codes", align_bytes=64)
+        lo_scales = keep.tile([P, NQ], U8, name="lo_scales", align_bytes=64)
+        quantize(lo_codes, lo_scales, lo, slice(0, NQ))
+        quantize(hi_codes, hi_scales, hi, slice(0, NQ))
+
+        k_grouped = keep.tile([P, N, PACK], BF16, name="k_grouped", align_bytes=64)
+        c_grouped = keep.tile([P, N, PACK], BF16, name="c_grouped", align_bytes=64)
+        k_codes = keep.tile([P, N], U32, name="k_codes", align_bytes=64)
+        k_scales = keep.tile([P, N], U8, name="k_scales", align_bytes=64)
+        c_codes = keep.tile([P, N], U32, name="c_codes", align_bytes=64)
+        c_scales = keep.tile([P, N], U8, name="c_scales", align_bytes=64)
+
+        halves = [slice(h * HALF, (h + 1) * HALF) for h in range(2)]
+        q_tiles = [slice(m * P, (m + 1) * P) for m in range(2)]
+        banks = [[psum.tile([P, HALF], F32, name="bank%d%d" % (h, m)) for m in range(2)] for h in range(2)]
+
+        def multiply(h, m, q_codes, q_scales, codes, scales, first):
+            nc.tensor.matmul_mx(
+                out=banks[h][m][:],
+                lhsT=q_codes[:, q_tiles[m]].bitcast(FP8X4),
+                lhsT_scale=q_scales[:, q_tiles[m]],
+                rhs=codes[:, halves[h]].bitcast(FP8X4),
+                rhs_scale=scales[:, halves[h]],
+                start=first,
+                stop=not first,
+            )
+
+        for t in range(PACK):
+            nc.vector.tensor_copy(k_grouped[:, :, t], k_planes[t][:].indirect(offsets[:]))
+        quantize(k_codes, k_scales, k_grouped, slice(0, N))
+        for h in range(2):
+            for m in range(2):
+                multiply(h, m, hi_codes, hi_scales, k_codes, k_scales, True)
+
+        for t in range(PACK - 1):
+            nc.vector.tensor_copy(c_grouped[:, :, t], c_planes[t][:].indirect(offsets[:]))
+        for h in range(2):
+            part = offsets[:, h * HALF // 16 : (h + 1) * HALF // 16]
+            nc.vector.tensor_copy(c_grouped[:, halves[h], PACK - 1], c_planes[PACK - 1][:].indirect(part))
+        for h in range(2):
+            quantize(c_codes, c_scales, c_grouped, halves[h])
+        for h in range(2):
+            for m in range(2):
+                multiply(h, m, lo_codes, lo_scales, c_codes, c_scales, False)
+                result = keep.tile([P, HALF], F32, name="result%d%d" % (h, m))
+                if m == 0:
+                    nc.scalar.copy(result[:], banks[h][m][:])
+                else:
+                    nc.vector.tensor_copy(result[:], banks[h][m][:])
+                nc.sync.dma_start(out=out[0, q_tiles[m], halves[h]], in_=result[:])

@@ -12,6 +12,7 @@ U16 = mybir.dt.uint16
 U8 = mybir.dt.uint8
 FP8X4 = mybir.dt.float8_e4m3fn_x4
 RELU = mybir.ActivationFunctionType.Relu
+COPY = mybir.ActivationFunctionType.Copy
 
 P = 128
 PACK = 4
@@ -35,8 +36,10 @@ def tile_attend_quest_f_topk_kernel(tc, qT, kT, cT, offs, out):
         nc.sync.dma_start(offsets[:], offs)
         for t in range(PACK):
             nc.sync.dma_start(out=k_planes[t][:], in_=k_rows[:, t, :])
-        for t in range(PACK):
+        for t in (2, 0, 1):
             nc.sync.dma_start(out=c_planes[t][:], in_=c_rows[:, t, :])
+        for cols in (slice(0, 1024), slice(1024, 1536), slice(1536, T)):
+            nc.sync.dma_start(out=c_planes[3][:, cols], in_=c_rows[:, 3, cols])
 
         def quantize(codes, scales, grouped, cols):
             nc.vector.quantize_mx(
@@ -86,11 +89,20 @@ def tile_attend_quest_f_topk_kernel(tc, qT, kT, cT, offs, out):
             for m in range(2):
                 multiply(h, m, hi_codes, hi_scales, k_codes, k_scales, True)
 
-        for t in range(PACK - 1):
+        parts = [offsets[:, h * HALF // 16 : (h + 1) * HALF // 16] for h in range(2)]
+        c2_half = keep.tile([P, T], BF16, name="c2_half")
+        c3_half = keep.tile([P, T], BF16, name="c3_half")
+        nc.vector.tensor_copy(c_grouped[:, halves[0], 2], c_planes[2][:].indirect(parts[0]))
+        nc.scalar.activation(c2_half[:], c_planes[2][:], COPY)
+        nc.scalar.activation(c_grouped[:, halves[1], 2], c2_half[:].indirect(parts[1]), COPY)
+        for t in (0, 1):
             nc.vector.tensor_copy(c_grouped[:, :, t], c_planes[t][:].indirect(offsets[:]))
-        for h in range(2):
-            part = offsets[:, h * HALF // 16 : (h + 1) * HALF // 16]
-            nc.vector.tensor_copy(c_grouped[:, halves[h], PACK - 1], c_planes[PACK - 1][:].indirect(part))
+        nc.scalar.activation(c3_half[:, 0:1024], c_planes[3][:, 0:1024], COPY)
+        nc.vector.tensor_copy(c3_half[:, 1024:1536], c_planes[3][:, 1024:1536])
+        nc.vector.tensor_copy(c3_half[:, 1536:1792], c_planes[3][:, 1536:1792])
+        nc.scalar.activation(c3_half[:, 1792:T], c_planes[3][:, 1792:T], COPY)
+        nc.vector.tensor_copy(c_grouped[:, halves[0], 3], c_planes[3][:].indirect(parts[0]))
+        nc.scalar.activation(c_grouped[:, halves[1], 3], c3_half[:].indirect(parts[1]), COPY)
         for h in range(2):
             quantize(c_codes, c_scales, c_grouped, halves[h])
         for h in range(2):

@@ -27,19 +27,20 @@ def tile_attend_quest_f_topk_kernel(tc, qT, kT, cT, offs, out):
 
         offsets = keep.tile([P, N // 16], U16, name="offsets")
         q_raw = keep.tile([P, PACK, NQ], F32, name="q_raw")
-        k_planes = [keep.tile([P, T], F32, name="k_plane%d" % t) for t in range(PACK)]
-        c_planes = [keep.tile([P, T], F32, name="c_plane%d" % t) for t in range(PACK)]
+        k_raw = keep.tile([P, PACK, T], F32, name="k_raw")
+        c_raw = keep.tile([P, PACK, T], F32, name="c_raw")
         k_rows = kT.rearrange("(p t) w -> p t w", t=PACK)
         c_rows = cT.rearrange("(p t) w -> p t w", t=PACK)
+        chunks = [slice(0, 896), slice(896, 1792), slice(1792, 2048)]
 
         nc.sync.dma_start(out=q_raw[:], in_=qT[0].rearrange("(p t) w -> p t w", t=PACK))
         nc.sync.dma_start(offsets[:], offs)
-        for t in range(PACK):
-            nc.sync.dma_start(out=k_planes[t][:], in_=k_rows[:, t, :])
-        for t in (2, 0, 1):
-            nc.sync.dma_start(out=c_planes[t][:], in_=c_rows[:, t, :])
-        for cols in (slice(0, 1024), slice(1024, 1536), slice(1536, T)):
-            nc.sync.dma_start(out=c_planes[3][:, cols], in_=c_rows[:, 3, cols])
+        nc.sync.dma_start(out=k_raw[:, 0:2, :], in_=k_rows[:, 0:2, :])
+        nc.sync.dma_start(out=k_raw[:, 2:4, :], in_=k_rows[:, 2:4, :])
+        nc.sync.dma_start(out=c_raw[:, 1:3, :], in_=c_rows[:, 1:3, :])
+        nc.sync.dma_start(out=c_raw[:, 0, :], in_=c_rows[:, 0, :])
+        for cols in chunks:
+            nc.sync.dma_start(out=c_raw[:, 3, cols], in_=c_rows[:, 3, cols])
 
         def quantize(codes, scales, grouped, cols):
             nc.vector.quantize_mx(
@@ -67,50 +68,52 @@ def tile_attend_quest_f_topk_kernel(tc, qT, kT, cT, offs, out):
         c_codes = keep.tile([P, N], U32, name="c_codes", align_bytes=64)
         c_scales = keep.tile([P, N], U8, name="c_scales", align_bytes=64)
 
-        halves = [slice(h * HALF, (h + 1) * HALF) for h in range(2)]
+        halves = [slice(0, HALF), slice(HALF, N)]
+        pieces = [slice(0, 128), slice(128, 256), slice(256, 512)]
         q_tiles = [slice(m * P, (m + 1) * P) for m in range(2)]
-        banks = [[psum.tile([P, HALF], F32, name="bank%d%d" % (h, m)) for m in range(2)] for h in range(2)]
+        banks = [[psum.tile([P, s.stop - s.start], F32, name="bank%d%d" % (h, m)) for m in range(2)] for h, s in enumerate(pieces)]
 
         def multiply(h, m, q_codes, q_scales, codes, scales, first):
             nc.tensor.matmul_mx(
                 out=banks[h][m][:],
                 lhsT=q_codes[:, q_tiles[m]].bitcast(FP8X4),
                 lhsT_scale=q_scales[:, q_tiles[m]],
-                rhs=codes[:, halves[h]].bitcast(FP8X4),
-                rhs_scale=scales[:, halves[h]],
+                rhs=codes[:, pieces[h]].bitcast(FP8X4),
+                rhs_scale=scales[:, pieces[h]],
                 start=first,
                 stop=not first,
             )
 
         for t in range(PACK):
-            nc.vector.tensor_copy(k_grouped[:, :, t], k_planes[t][:].indirect(offsets[:]))
+            nc.vector.tensor_copy(k_grouped[:, :, t], k_raw[:, t, :].indirect(offsets[:]))
         quantize(k_codes, k_scales, k_grouped, slice(0, N))
-        for h in range(2):
+        for h in range(3):
             for m in range(2):
                 multiply(h, m, hi_codes, hi_scales, k_codes, k_scales, True)
 
         parts = [offsets[:, h * HALF // 16 : (h + 1) * HALF // 16] for h in range(2)]
         c2_half = keep.tile([P, T], BF16, name="c2_half")
         c3_half = keep.tile([P, T], BF16, name="c3_half")
-        nc.vector.tensor_copy(c_grouped[:, halves[0], 2], c_planes[2][:].indirect(parts[0]))
-        nc.scalar.activation(c2_half[:], c_planes[2][:], COPY)
+        nc.vector.tensor_copy(c_grouped[:, :, 1], c_raw[:, 1, :].indirect(offsets[:]))
+        nc.vector.tensor_copy(c_grouped[:, halves[0], 2], c_raw[:, 2, :].indirect(parts[0]))
+        nc.scalar.activation(c2_half[:], c_raw[:, 2, :], COPY)
         nc.scalar.activation(c_grouped[:, halves[1], 2], c2_half[:].indirect(parts[1]), COPY)
-        for t in (0, 1):
-            nc.vector.tensor_copy(c_grouped[:, :, t], c_planes[t][:].indirect(offsets[:]))
-        nc.scalar.activation(c3_half[:, 0:1024], c_planes[3][:, 0:1024], COPY)
-        nc.vector.tensor_copy(c3_half[:, 1024:1536], c_planes[3][:, 1024:1536])
-        nc.vector.tensor_copy(c3_half[:, 1536:1792], c_planes[3][:, 1536:1792])
-        nc.scalar.activation(c3_half[:, 1792:T], c_planes[3][:, 1792:T], COPY)
-        nc.vector.tensor_copy(c_grouped[:, halves[0], 3], c_planes[3][:].indirect(parts[0]))
+        nc.vector.tensor_copy(c_grouped[:, :, 0], c_raw[:, 0, :].indirect(offsets[:]))
+        nc.scalar.activation(c3_half[:, 0:896], c_raw[:, 3, 0:896], COPY)
+        nc.scalar.activation(c3_half[:, 896:1152], c_raw[:, 3, 896:1152], COPY)
+        nc.vector.tensor_copy(c3_half[:, 1152:1792], c_raw[:, 3, 1152:1792])
+        nc.vector.tensor_copy(c3_half[:, 1792:1920], c_raw[:, 3, 1792:1920])
+        nc.scalar.activation(c3_half[:, 1920:2048], c_raw[:, 3, 1920:2048], COPY)
+        nc.vector.tensor_copy(c_grouped[:, halves[0], 3], c_raw[:, 3, :].indirect(parts[0]))
         nc.scalar.activation(c_grouped[:, halves[1], 3], c3_half[:].indirect(parts[1]), COPY)
-        for h in range(2):
-            quantize(c_codes, c_scales, c_grouped, halves[h])
-        for h in range(2):
+        for h in range(3):
+            quantize(c_codes, c_scales, c_grouped, pieces[h])
+        for h in range(3):
             for m in range(2):
                 multiply(h, m, lo_codes, lo_scales, c_codes, c_scales, False)
-                result = keep.tile([P, HALF], F32, name="result%d%d" % (h, m))
-                if m == 0:
-                    nc.scalar.copy(result[:], banks[h][m][:])
-                else:
+                result = keep.tile([P, pieces[h].stop - pieces[h].start], F32, name="result%d%d" % (h, m))
+                if (h, m) in ((1, 0), (2, 1)):
                     nc.vector.tensor_copy(result[:], banks[h][m][:])
-                nc.sync.dma_start(out=out[0, q_tiles[m], halves[h]], in_=result[:])
+                else:
+                    nc.scalar.copy(result[:], banks[h][m][:])
+                nc.sync.dma_start(out=out[0, q_tiles[m], pieces[h]], in_=result[:])

@@ -102,8 +102,7 @@ def tile_attend_quest_f_topk_kernel(tc, qT, kT, cT, offs, out):
         nc.scalar.activation(c3_half[:, 0:896], c_raw[:, 3, 0:896], COPY)
         nc.scalar.activation(c3_half[:, 896:1152], c_raw[:, 3, 896:1152], COPY)
         nc.vector.tensor_copy(c3_half[:, 1152:1792], c_raw[:, 3, 1152:1792])
-        nc.vector.tensor_copy(c3_half[:, 1792:1920], c_raw[:, 3, 1792:1920])
-        nc.scalar.activation(c3_half[:, 1920:2048], c_raw[:, 3, 1920:2048], COPY)
+        nc.scalar.activation(c3_half[:, 1792:2048], c_raw[:, 3, 1792:2048], COPY)
         nc.vector.tensor_copy(c_grouped[:, halves[0], 3], c_raw[:, 3, :].indirect(parts[0]))
         nc.scalar.activation(c_grouped[:, halves[1], 3], c3_half[:].indirect(parts[1]), COPY)
         for h in range(3):

@@ -111,7 +111,7 @@ def tile_attend_quest_f_topk_kernel(tc, qT, kT, cT, offs, out):
             for m in range(2):
                 multiply(h, m, lo_codes, lo_scales, c_codes, c_scales, False)
                 result = keep.tile([P, pieces[h].stop - pieces[h].start], F32, name="result%d%d" % (h, m))
-                if (h, m) in ((1, 0), (2, 1)):
+                if (h, m) == (2, 1):
                     nc.vector.tensor_copy(result[:], banks[h][m][:])
                 else:
                     nc.scalar.copy(result[:], banks[h][m][:])

@@ -37,8 +37,8 @@ def tile_attend_quest_f_topk_kernel(tc, qT, kT, cT, offs, out):
         nc.sync.dma_start(offsets[:], offs)
         nc.sync.dma_start(out=k_raw[:, 0:2, :], in_=k_rows[:, 0:2, :])
         nc.sync.dma_start(out=k_raw[:, 2:4, :], in_=k_rows[:, 2:4, :])
-        nc.sync.dma_start(out=c_raw[:, 1:3, :], in_=c_rows[:, 1:3, :])
-        nc.sync.dma_start(out=c_raw[:, 0, :], in_=c_rows[:, 0, :])
+        for t in (2, 1, 0):
+            nc.sync.dma_start(out=c_raw[:, t, :], in_=c_rows[:, t, :])
         for cols in chunks:
             nc.sync.dma_start(out=c_raw[:, 3, cols], in_=c_rows[:, 3, cols])
 
@@ -84,20 +84,26 @@ def tile_attend_quest_f_topk_kernel(tc, qT, kT, cT, offs, out):
                 stop=not first,
             )
 
-        for t in range(PACK):
+        parts = [offsets[:, h * HALF // 16 : (h + 1) * HALF // 16] for h in range(2)]
+        for t in range(2):
             nc.vector.tensor_copy(k_grouped[:, :, t], k_raw[:, t, :].indirect(offsets[:]))
+        picked = keep.tile([P, 2, HALF], F32, name="picked")
+        for t in range(2):
+            nc.vector.tensor_copy(picked[:, t, :], k_raw[:, 2 + t, :].indirect(parts[1]))
+        nc.scalar.activation(k_grouped[:, halves[1], 2:4], picked[:].rearrange("p t n -> p n t"), COPY)
+        for t in range(2, PACK):
+            nc.vector.tensor_copy(k_grouped[:, halves[0], t], k_raw[:, t, :].indirect(parts[0]))
         quantize(k_codes, k_scales, k_grouped, slice(0, N))
         for h in range(3):
             for m in range(2):
                 multiply(h, m, hi_codes, hi_scales, k_codes, k_scales, True)
 
-        parts = [offsets[:, h * HALF // 16 : (h + 1) * HALF // 16] for h in range(2)]
         c2_half = keep.tile([P, T], BF16, name="c2_half")
         c3_half = keep.tile([P, T], BF16, name="c3_half")
-        nc.vector.tensor_copy(c_grouped[:, :, 1], c_raw[:, 1, :].indirect(offsets[:]))
         nc.vector.tensor_copy(c_grouped[:, halves[0], 2], c_raw[:, 2, :].indirect(parts[0]))
         nc.scalar.activation(c2_half[:], c_raw[:, 2, :], COPY)
         nc.scalar.activation(c_grouped[:, halves[1], 2], c2_half[:].indirect(parts[1]), COPY)
+        nc.vector.tensor_copy(c_grouped[:, :, 1], c_raw[:, 1, :].indirect(offsets[:]))
         nc.vector.tensor_copy(c_grouped[:, :, 0], c_raw[:, 0, :].indirect(offsets[:]))
         nc.scalar.activation(c3_half[:, 0:896], c_raw[:, 3, 0:896], COPY)
         nc.scalar.activation(c3_half[:, 896:1152], c_raw[:, 3, 896:1152], COPY)

@@ -69,17 +69,19 @@ def tile_attend_quest_f_topk_kernel(tc, qT, kT, cT, offs, out):
         c_scales = keep.tile([P, N], U8, name="c_scales", align_bytes=64)
 
         halves = [slice(0, HALF), slice(HALF, N)]
-        pieces = [slice(0, 128), slice(128, 256), slice(256, 512)]
+        quarters = [slice(h * P, (h + 1) * P) for h in range(N // P)]
         q_tiles = [slice(m * P, (m + 1) * P) for m in range(2)]
-        banks = [[psum.tile([P, s.stop - s.start], F32, name="bank%d%d" % (h, m)) for m in range(2)] for h, s in enumerate(pieces)]
+        groups = [(m, cols) for h in range(2) for m, cols in ((0, quarters[2 * h]), (0, quarters[2 * h + 1]), (1, halves[h]))]
+        banks = [psum.tile([P, cols.stop - cols.start], F32, name="bank%d" % g) for g, (m, cols) in enumerate(groups)]
 
-        def multiply(h, m, q_codes, q_scales, codes, scales, first):
+        def multiply(g, q_codes, q_scales, codes, scales, first):
+            m, cols = groups[g]
             nc.tensor.matmul_mx(
-                out=banks[h][m][:],
+                out=banks[g][:],
                 lhsT=q_codes[:, q_tiles[m]].bitcast(FP8X4),
                 lhsT_scale=q_scales[:, q_tiles[m]],
-                rhs=codes[:, pieces[h]].bitcast(FP8X4),
-                rhs_scale=scales[:, pieces[h]],
+                rhs=codes[:, cols].bitcast(FP8X4),
+                rhs_scale=scales[:, cols],
                 start=first,
                 stop=not first,
             )
@@ -94,9 +96,8 @@ def tile_attend_quest_f_topk_kernel(tc, qT, kT, cT, offs, out):
         for t in range(2, PACK):
             nc.vector.tensor_copy(k_grouped[:, halves[0], t], k_raw[:, t, :].indirect(parts[0]))
         quantize(k_codes, k_scales, k_grouped, slice(0, N))
-        for h in range(3):
-            for m in range(2):
-                multiply(h, m, hi_codes, hi_scales, k_codes, k_scales, True)
+        for g in range(len(groups)):
+            multiply(g, hi_codes, hi_scales, k_codes, k_scales, True)
 
         c2_half = keep.tile([P, T], BF16, name="c2_half")
         c3_half = keep.tile([P, T], BF16, name="c3_half")
@@ -111,14 +112,15 @@ def tile_attend_quest_f_topk_kernel(tc, qT, kT, cT, offs, out):
         nc.scalar.activation(c3_half[:, 1792:2048], c_raw[:, 3, 1792:2048], COPY)
         nc.vector.tensor_copy(c_grouped[:, halves[0], 3], c_raw[:, 3, :].indirect(parts[0]))
         nc.scalar.activation(c_grouped[:, halves[1], 3], c3_half[:].indirect(parts[1]), COPY)
-        for h in range(3):
-            quantize(c_codes, c_scales, c_grouped, pieces[h])
-        for h in range(3):
-            for m in range(2):
-                multiply(h, m, lo_codes, lo_scales, c_codes, c_scales, False)
-                result = keep.tile([P, pieces[h].stop - pieces[h].start], F32, name="result%d%d" % (h, m))
-                if (h, m) == (2, 1):
-                    nc.vector.tensor_copy(result[:], banks[h][m][:])
-                else:
-                    nc.scalar.copy(result[:], banks[h][m][:])
-                nc.sync.dma_start(out=out[0, q_tiles[m], pieces[h]], in_=result[:])
+        for cols in quarters:
+            quantize(c_codes, c_scales, c_grouped, cols)
+        results = [keep.tile([P, N], F32, name="result%d" % m) for m in range(2)]
+        for g, (m, cols) in enumerate(groups):
+            multiply(g, lo_codes, lo_scales, c_codes, c_scales, False)
+            if m == 0 and cols.start >= HALF:
+                nc.vector.tensor_copy(results[m][:, cols], banks[g][:])
+            else:
+                nc.scalar.copy(results[m][:, cols], banks[g][:])
+            if cols.stop % HALF == 0:
+                half = halves[cols.start // HALF]
+                nc.sync.dma_start(out=out[0, q_tiles[m], half], in_=results[m][:, half])

@@ -109,7 +109,8 @@ def tile_attend_quest_f_topk_kernel(tc, qT, kT, cT, offs, out):
         nc.scalar.activation(c3_half[:, 0:896], c_raw[:, 3, 0:896], COPY)
         nc.scalar.activation(c3_half[:, 896:1152], c_raw[:, 3, 896:1152], COPY)
         nc.vector.tensor_copy(c3_half[:, 1152:1792], c_raw[:, 3, 1152:1792])
-        nc.scalar.activation(c3_half[:, 1792:2048], c_raw[:, 3, 1792:2048], COPY)
+        nc.vector.tensor_copy(c3_half[:, 1792:1920], c_raw[:, 3, 1792:1920])
+        nc.scalar.activation(c3_half[:, 1920:2048], c_raw[:, 3, 1920:2048], COPY)
         nc.vector.tensor_copy(c_grouped[:, halves[0], 3], c_raw[:, 3, :].indirect(parts[0]))
         nc.scalar.activation(c_grouped[:, halves[1], 3], c3_half[:].indirect(parts[1]), COPY)
         for cols in quarters:

@@ -28,7 +28,7 @@ def tile_attend_quest_f_topk_kernel(tc, qT, kT, cT, offs, out):
         offsets = keep.tile([P, N // 16], U16, name="offsets")
         q_raw = keep.tile([P, PACK, NQ], F32, name="q_raw")
         k_raw = keep.tile([P, PACK, T], F32, name="k_raw")
-        c_raw = keep.tile([P, PACK, T], F32, name="c_raw")
+        c_raw = [keep.tile([P, T], F32, name="c_raw%d" % t, tag="c_raw%d" % t, align_bytes=64) for t in range(PACK)]
         k_rows = kT.rearrange("(p t) w -> p t w", t=PACK)
         c_rows = cT.rearrange("(p t) w -> p t w", t=PACK)
         chunks = [slice(0, 896), slice(896, 1792), slice(1792, 2048)]
@@ -38,9 +38,9 @@ def tile_attend_quest_f_topk_kernel(tc, qT, kT, cT, offs, out):
         nc.sync.dma_start(out=k_raw[:, 0:2, :], in_=k_rows[:, 0:2, :])
         nc.sync.dma_start(out=k_raw[:, 2:4, :], in_=k_rows[:, 2:4, :])
         for t in (2, 1, 0):
-            nc.sync.dma_start(out=c_raw[:, t, :], in_=c_rows[:, t, :])
+            nc.sync.dma_start(out=c_raw[t][:, :], in_=c_rows[:, t, :])
         for cols in chunks:
-            nc.sync.dma_start(out=c_raw[:, 3, cols], in_=c_rows[:, 3, cols])
+            nc.sync.dma_start(out=c_raw[3][:, cols], in_=c_rows[:, 3, cols])
 
         def quantize(codes, scales, grouped, cols):
             nc.vector.quantize_mx(
@@ -54,12 +54,9 @@ def tile_attend_quest_f_topk_kernel(tc, qT, kT, cT, offs, out):
         lo = keep.tile([P, NQ, PACK], BF16, name="lo", align_bytes=64)
         nc.scalar.activation(hi[:], q_view, RELU)
         nc.vector.tensor_scalar_min(lo[:], q_view, 0.0)
-        hi_codes = keep.tile([P, NQ], U32, name="hi_codes", align_bytes=64)
-        hi_scales = keep.tile([P, NQ], U8, name="hi_scales", align_bytes=64)
         lo_codes = keep.tile([P, NQ], U32, name="lo_codes", align_bytes=64)
         lo_scales = keep.tile([P, NQ], U8, name="lo_scales", align_bytes=64)
         quantize(lo_codes, lo_scales, lo, slice(0, NQ))
-        quantize(hi_codes, hi_scales, hi, slice(0, NQ))
 
         k_grouped = keep.tile([P, N, PACK], BF16, name="k_grouped", align_bytes=64)
         c_grouped = keep.tile([P, N, PACK], BF16, name="c_grouped", align_bytes=64)
@@ -74,7 +71,7 @@ def tile_attend_quest_f_topk_kernel(tc, qT, kT, cT, offs, out):
         groups = [(m, cols) for h in range(2) for m, cols in ((0, quarters[2 * h]), (0, quarters[2 * h + 1]), (1, halves[h]))]
         banks = [psum.tile([P, cols.stop - cols.start], F32, name="bank%d" % g) for g, (m, cols) in enumerate(groups)]
 
-        def multiply(g, q_codes, q_scales, codes, scales, first):
+        def multiply(g, q_codes, q_scales, codes, scales, start, stop):
             m, cols = groups[g]
             nc.tensor.matmul_mx(
                 out=banks[g][:],
@@ -82,8 +79,8 @@ def tile_attend_quest_f_topk_kernel(tc, qT, kT, cT, offs, out):
                 lhsT_scale=q_scales[:, q_tiles[m]],
                 rhs=codes[:, cols].bitcast(FP8X4),
                 rhs_scale=scales[:, cols],
-                start=first,
-                stop=not first,
+                start=start,
+                stop=stop,
             )
 
         parts = [offsets[:, h * HALF // 16 : (h + 1) * HALF // 16] for h in range(2)]
@@ -96,28 +93,34 @@ def tile_attend_quest_f_topk_kernel(tc, qT, kT, cT, offs, out):
         for t in range(2, PACK):
             nc.vector.tensor_copy(k_grouped[:, halves[0], t], k_raw[:, t, :].indirect(parts[0]))
         quantize(k_codes, k_scales, k_grouped, slice(0, N))
-        for g in range(len(groups)):
-            multiply(g, hi_codes, hi_scales, k_codes, k_scales, True)
 
         c2_half = keep.tile([P, T], BF16, name="c2_half")
         c3_half = keep.tile([P, T], BF16, name="c3_half")
-        nc.vector.tensor_copy(c_grouped[:, halves[0], 2], c_raw[:, 2, :].indirect(parts[0]))
-        nc.scalar.activation(c2_half[:], c_raw[:, 2, :], COPY)
+        nc.vector.tensor_copy(c_grouped[:, halves[0], 2], c_raw[2][:, :].indirect(parts[0]))
+        nc.scalar.activation(c2_half[:], c_raw[2][:, :], COPY)
         nc.scalar.activation(c_grouped[:, halves[1], 2], c2_half[:].indirect(parts[1]), COPY)
-        nc.vector.tensor_copy(c_grouped[:, :, 1], c_raw[:, 1, :].indirect(offsets[:]))
-        nc.vector.tensor_copy(c_grouped[:, :, 0], c_raw[:, 0, :].indirect(offsets[:]))
-        nc.scalar.activation(c3_half[:, 0:896], c_raw[:, 3, 0:896], COPY)
-        nc.scalar.activation(c3_half[:, 896:1152], c_raw[:, 3, 896:1152], COPY)
-        nc.vector.tensor_copy(c3_half[:, 1152:1792], c_raw[:, 3, 1152:1792])
-        nc.vector.tensor_copy(c3_half[:, 1792:1920], c_raw[:, 3, 1792:1920])
-        nc.scalar.activation(c3_half[:, 1920:2048], c_raw[:, 3, 1920:2048], COPY)
-        nc.vector.tensor_copy(c_grouped[:, halves[0], 3], c_raw[:, 3, :].indirect(parts[0]))
+        nc.vector.tensor_copy(c_grouped[:, :, 1], c_raw[1][:, :].indirect(offsets[:]))
+        nc.vector.tensor_copy(c_grouped[:, :, 0], c_raw[0][:, :].indirect(offsets[:]))
+        hi_codes = keep.tile([P, NQ], U32, name="hi_codes", tag="c_raw0", align_bytes=64)
+        hi_scales = keep.tile([P, NQ], U8, name="hi_scales", align_bytes=64)
+        quantize(hi_codes, hi_scales, hi, slice(0, NQ))
+        for g, (m, cols) in enumerate(groups):
+            if m == 1:
+                multiply(g, hi_codes, hi_scales, k_codes, k_scales, True, True)
+        for g in range(len(groups)):
+            multiply(g, hi_codes, hi_scales, k_codes, k_scales, True, False)
+        nc.scalar.activation(c3_half[:, 0:896], c_raw[3][:, 0:896], COPY)
+        nc.scalar.activation(c3_half[:, 896:1152], c_raw[3][:, 896:1152], COPY)
+        nc.vector.tensor_copy(c3_half[:, 1152:1792], c_raw[3][:, 1152:1792])
+        nc.vector.tensor_copy(c3_half[:, 1792:1920], c_raw[3][:, 1792:1920])
+        nc.scalar.activation(c3_half[:, 1920:2048], c_raw[3][:, 1920:2048], COPY)
+        nc.vector.tensor_copy(c_grouped[:, halves[0], 3], c_raw[3][:, :].indirect(parts[0]))
         nc.scalar.activation(c_grouped[:, halves[1], 3], c3_half[:].indirect(parts[1]), COPY)
         for cols in quarters:
             quantize(c_codes, c_scales, c_grouped, cols)
         results = [keep.tile([P, N], F32, name="result%d" % m) for m in range(2)]
         for g, (m, cols) in enumerate(groups):
-            multiply(g, lo_codes, lo_scales, c_codes, c_scales, False)
+            multiply(g, lo_codes, lo_scales, c_codes, c_scales, False, True)
             if m == 0 and cols.start >= HALF:
                 nc.vector.tensor_copy(results[m][:, cols], banks[g][:])
             else:

@@ -8,6 +8,7 @@ FLOPS = 2 * 2 * NQ * D * N
 F32 = mybir.dt.float32
 BF16 = mybir.dt.bfloat16
 U32 = mybir.dt.uint32
+I32 = mybir.dt.int32
 U16 = mybir.dt.uint16
 U8 = mybir.dt.uint8
 FP8X4 = mybir.dt.float8_e4m3fn_x4
@@ -57,6 +58,10 @@ def tile_attend_quest_f_topk_kernel(tc, qT, kT, cT, offs, out):
         lo_codes = keep.tile([P, NQ], U32, name="lo_codes", align_bytes=64)
         lo_scales = keep.tile([P, NQ], U8, name="lo_scales", align_bytes=64)
         quantize(lo_codes, lo_scales, lo, slice(0, NQ))
+        hi_codes = keep.tile([P, NQ], U32, name="hi_codes", align_bytes=64)
+        hi_made = keep.tile([P, NQ], U8, name="hi_made", align_bytes=64)
+        nc.vector.memset(hi_made[:].bitcast(I32), 0)
+        quantize(hi_codes, hi_made, hi, slice(0, NQ))
 
         k_grouped = keep.tile([P, N, PACK], BF16, name="k_grouped", align_bytes=64)
         c_grouped = keep.tile([P, N, PACK], BF16, name="c_grouped", align_bytes=64)
@@ -101,9 +106,8 @@ def tile_attend_quest_f_topk_kernel(tc, qT, kT, cT, offs, out):
         nc.scalar.activation(c_grouped[:, halves[1], 2], c2_half[:].indirect(parts[1]), COPY)
         nc.vector.tensor_copy(c_grouped[:, :, 1], c_raw[1][:, :].indirect(offsets[:]))
         nc.vector.tensor_copy(c_grouped[:, :, 0], c_raw[0][:, :].indirect(offsets[:]))
-        hi_codes = keep.tile([P, NQ], U32, name="hi_codes", tag="c_raw0", align_bytes=64)
-        hi_scales = keep.tile([P, NQ], U8, name="hi_scales", align_bytes=64)
-        quantize(hi_codes, hi_scales, hi, slice(0, NQ))
+        hi_scales = keep.tile([P, NQ], U8, name="hi_scales", tag="c_raw0", align_bytes=64)
+        nc.gpsimd.tensor_copy(hi_scales[:].bitcast(I32), hi_made[:].bitcast(I32))
         for g, (m, cols) in enumerate(groups):
             if m == 1:
                 multiply(g, hi_codes, hi_scales, k_codes, k_scales, True, True)

@@ -106,7 +106,7 @@ def tile_attend_quest_f_topk_kernel(tc, qT, kT, cT, offs, out):
         nc.scalar.activation(c_grouped[:, halves[1], 2], c2_half[:].indirect(parts[1]), COPY)
         nc.vector.tensor_copy(c_grouped[:, :, 1], c_raw[1][:, :].indirect(offsets[:]))
         nc.vector.tensor_copy(c_grouped[:, :, 0], c_raw[0][:, :].indirect(offsets[:]))
-        hi_scales = keep.tile([P, NQ], U8, name="hi_scales", tag="c_raw0", align_bytes=64)
+        hi_scales = keep.tile([P, NQ], U8, name="hi_scales", tag="c_raw1", align_bytes=64)
         nc.gpsimd.tensor_copy(hi_scales[:].bitcast(I32), hi_made[:].bitcast(I32))
         for g, (m, cols) in enumerate(groups):
             if m == 1:

@@ -110,7 +110,17 @@ def tile_attend_quest_f_topk_kernel(tc, qT, kT, cT, offs, out):
         nc.gpsimd.tensor_copy(hi_scales[:].bitcast(I32), hi_made[:].bitcast(I32))
         for g, (m, cols) in enumerate(groups):
             if m == 1:
-                multiply(g, hi_codes, hi_scales, k_codes, k_scales, True, True)
+                for first in range(0, HALF, 64):
+                    slots = slice(cols.start + first, cols.start + first + 64)
+                    nc.tensor.matmul_mx(
+                        out=banks[g][:, first : first + 64],
+                        lhsT=hi_codes[:, q_tiles[m]].bitcast(FP8X4),
+                        lhsT_scale=hi_scales[:, q_tiles[m]],
+                        rhs=k_codes[:, slots].bitcast(FP8X4),
+                        rhs_scale=k_scales[:, slots],
+                        start=True,
+                        stop=True,
+                    )
         for g in range(len(groups)):
             multiply(g, hi_codes, hi_scales, k_codes, k_scales, True, False)
         nc.scalar.activation(c3_half[:, 0:896], c_raw[3][:, 0:896], COPY)

@@ -73,7 +73,7 @@ def tile_attend_quest_f_topk_kernel(tc, qT, kT, cT, offs, out):
         halves = [slice(0, HALF), slice(HALF, N)]
         quarters = [slice(h * P, (h + 1) * P) for h in range(N // P)]
         q_tiles = [slice(m * P, (m + 1) * P) for m in range(2)]
-        groups = [(m, cols) for h in range(2) for m, cols in ((0, quarters[2 * h]), (0, quarters[2 * h + 1]), (1, halves[h]))]
+        groups = [(0, quarters[0]), (0, quarters[1]), (1, halves[0])] + [(m, cols) for cols in quarters[2:] for m in range(2)]
         banks = [psum.tile([P, cols.stop - cols.start], F32, name="bank%d" % g) for g, (m, cols) in enumerate(groups)]
 
         def multiply(g, q_codes, q_scales, codes, scales, start, stop):
@@ -110,7 +110,7 @@ def tile_attend_quest_f_topk_kernel(tc, qT, kT, cT, offs, out):
         nc.gpsimd.tensor_copy(hi_scales[:].bitcast(I32), hi_made[:].bitcast(I32))
         for g, (m, cols) in enumerate(groups):
             if m == 1:
-                for first in range(0, HALF, 64):
+                for first in range(0, cols.stop - cols.start, 64):
                     slots = slice(cols.start + first, cols.start + first + 64)
                     nc.tensor.matmul_mx(
                         out=banks[g][:, first : first + 64],

@@ -126,8 +126,7 @@ def tile_attend_quest_f_topk_kernel(tc, qT, kT, cT, offs, out):
         nc.scalar.activation(c3_half[:, 0:896], c_raw[3][:, 0:896], COPY)
         nc.scalar.activation(c3_half[:, 896:1152], c_raw[3][:, 896:1152], COPY)
         nc.vector.tensor_copy(c3_half[:, 1152:1792], c_raw[3][:, 1152:1792])
-        nc.vector.tensor_copy(c3_half[:, 1792:1920], c_raw[3][:, 1792:1920])
-        nc.scalar.activation(c3_half[:, 1920:2048], c_raw[3][:, 1920:2048], COPY)
+        nc.scalar.activation(c3_half[:, 1792:2048], c_raw[3][:, 1792:2048], COPY)
         nc.vector.tensor_copy(c_grouped[:, halves[0], 3], c_raw[3][:, :].indirect(parts[0]))
         nc.scalar.activation(c_grouped[:, halves[1], 3], c3_half[:].indirect(parts[1]), COPY)
         for cols in quarters:
@@ -139,6 +138,8 @@ def tile_attend_quest_f_topk_kernel(tc, qT, kT, cT, offs, out):
                 nc.vector.tensor_copy(results[m][:, cols], banks[g][:])
             else:
                 nc.scalar.copy(results[m][:, cols], banks[g][:])
-            if cols.stop % HALF == 0:
+            if g < 2:
+                nc.sync.dma_start(out=out[0, q_tiles[m], cols], in_=results[m][:, cols])
+            elif cols.stop % HALF == 0:
                 half = halves[cols.start // HALF]
                 nc.sync.dma_start(out=out[0, q_tiles[m], half], in_=results[m][:, half])

@@ -8,7 +8,6 @@ FLOPS = 2 * 2 * NQ * D * N
 F32 = mybir.dt.float32
 BF16 = mybir.dt.bfloat16
 U32 = mybir.dt.uint32
-I32 = mybir.dt.int32
 U16 = mybir.dt.uint16
 U8 = mybir.dt.uint8
 FP8X4 = mybir.dt.float8_e4m3fn_x4
@@ -58,10 +57,9 @@ def tile_attend_quest_f_topk_kernel(tc, qT, kT, cT, offs, out):
         lo_codes = keep.tile([P, NQ], U32, name="lo_codes", align_bytes=64)
         lo_scales = keep.tile([P, NQ], U8, name="lo_scales", align_bytes=64)
         quantize(lo_codes, lo_scales, lo, slice(0, NQ))
-        hi_codes = keep.tile([P, NQ], U32, name="hi_codes", align_bytes=64)
-        hi_made = keep.tile([P, NQ], U8, name="hi_made", align_bytes=64)
-        nc.vector.memset(hi_made[:].bitcast(I32), 0)
-        quantize(hi_codes, hi_made, hi, slice(0, NQ))
+        hi_made = keep.tile([P, NQ], U32, name="hi_made", align_bytes=64)
+        hi_scales = keep.tile([P, NQ], U8, name="hi_scales", align_bytes=64)
+        quantize(hi_made, hi_scales, hi, slice(0, NQ))
 
         k_grouped = keep.tile([P, N, PACK], BF16, name="k_grouped", align_bytes=64)
         c_grouped = keep.tile([P, N, PACK], BF16, name="c_grouped", align_bytes=64)
@@ -106,8 +104,8 @@ def tile_attend_quest_f_topk_kernel(tc, qT, kT, cT, offs, out):
         nc.scalar.activation(c_grouped[:, halves[1], 2], c2_half[:].indirect(parts[1]), COPY)
         nc.vector.tensor_copy(c_grouped[:, :, 1], c_raw[1][:, :].indirect(offsets[:]))
         nc.vector.tensor_copy(c_grouped[:, :, 0], c_raw[0][:, :].indirect(offsets[:]))
-        hi_scales = keep.tile([P, NQ], U8, name="hi_scales", tag="c_raw1", align_bytes=64)
-        nc.gpsimd.tensor_copy(hi_scales[:].bitcast(I32), hi_made[:].bitcast(I32))
+        hi_codes = keep.tile([P, NQ], U32, name="hi_codes", tag="c_raw1", align_bytes=64)
+        nc.gpsimd.tensor_copy(hi_codes[:], hi_made[:])
         for g, (m, cols) in enumerate(groups):
             if m == 1:
                 for first in range(0, cols.stop - cols.start, 64):

@@ -31,7 +31,7 @@ def tile_attend_quest_f_topk_kernel(tc, qT, kT, cT, offs, out):
         c_raw = [keep.tile([P, T], F32, name="c_raw%d" % t, tag="c_raw%d" % t, align_bytes=64) for t in range(PACK)]
         k_rows = kT.rearrange("(p t) w -> p t w", t=PACK)
         c_rows = cT.rearrange("(p t) w -> p t w", t=PACK)
-        chunks = [slice(0, 896), slice(896, 1792), slice(1792, 2048)]
+        chunks = [slice(0, 1088), slice(1088, 1792), slice(1792, 2048)]
 
         nc.sync.dma_start(out=q_raw[:], in_=qT[0].rearrange("(p t) w -> p t w", t=PACK))
         nc.sync.dma_start(offsets[:], offs)
@@ -121,9 +121,10 @@ def tile_attend_quest_f_topk_kernel(tc, qT, kT, cT, offs, out):
                     )
         for g in range(len(groups)):
             multiply(g, hi_codes, hi_scales, k_codes, k_scales, True, False)
-        nc.scalar.activation(c3_half[:, 0:896], c_raw[3][:, 0:896], COPY)
-        nc.scalar.activation(c3_half[:, 896:1152], c_raw[3][:, 896:1152], COPY)
-        nc.vector.tensor_copy(c3_half[:, 1152:1792], c_raw[3][:, 1152:1792])
+        nc.scalar.activation(c3_half[:, 0:768], c_raw[3][:, 0:768], COPY)
+        nc.vector.tensor_copy(c3_half[:, 768:1088], c_raw[3][:, 768:1088])
+        nc.scalar.activation(c3_half[:, 1088:1344], c_raw[3][:, 1088:1344], COPY)
+        nc.vector.tensor_copy(c3_half[:, 1344:1792], c_raw[3][:, 1344:1792])
         nc.scalar.activation(c3_half[:, 1792:2048], c_raw[3][:, 1792:2048], COPY)
         nc.vector.tensor_copy(c_grouped[:, halves[0], 3], c_raw[3][:, :].indirect(parts[0]))
         nc.scalar.activation(c_grouped[:, halves[1], 3], c3_half[:].indirect(parts[1]), COPY)

@@ -106,19 +106,17 @@ def tile_attend_quest_f_topk_kernel(tc, qT, kT, cT, offs, out):
         nc.vector.tensor_copy(c_grouped[:, :, 0], c_raw[0][:, :].indirect(offsets[:]))
         hi_codes = keep.tile([P, NQ], U32, name="hi_codes", tag="c_raw1", align_bytes=64)
         nc.gpsimd.tensor_copy(hi_codes[:], hi_made[:])
-        for g, (m, cols) in enumerate(groups):
-            if m == 1:
-                for first in range(0, cols.stop - cols.start, 64):
-                    slots = slice(cols.start + first, cols.start + first + 64)
-                    nc.tensor.matmul_mx(
-                        out=banks[g][:, first : first + 64],
-                        lhsT=hi_codes[:, q_tiles[m]].bitcast(FP8X4),
-                        lhsT_scale=hi_scales[:, q_tiles[m]],
-                        rhs=k_codes[:, slots].bitcast(FP8X4),
-                        rhs_scale=k_scales[:, slots],
-                        start=True,
-                        stop=True,
-                    )
+        spare = psum.tile([P, N], F32, name="spare")
+        for repeat in range(3):
+            nc.tensor.matmul_mx(
+                out=spare[0:32, :],
+                lhsT=hi_codes[:, 0:32].bitcast(FP8X4),
+                lhsT_scale=hi_scales[:, 0:32],
+                rhs=k_codes[:].bitcast(FP8X4),
+                rhs_scale=k_scales[:],
+                start=True,
+                stop=True,
+            )
         for g in range(len(groups)):
             multiply(g, hi_codes, hi_scales, k_codes, k_scales, True, False)
         nc.scalar.activation(c3_half[:, 0:768], c_raw[3][:, 0:768], COPY)

@@ -8,6 +8,7 @@ FLOPS = 2 * 2 * NQ * D * N
 F32 = mybir.dt.float32
 BF16 = mybir.dt.bfloat16
 U32 = mybir.dt.uint32
+I32 = mybir.dt.int32
 U16 = mybir.dt.uint16
 U8 = mybir.dt.uint8
 FP8X4 = mybir.dt.float8_e4m3fn_x4
@@ -57,9 +58,10 @@ def tile_attend_quest_f_topk_kernel(tc, qT, kT, cT, offs, out):
         lo_codes = keep.tile([P, NQ], U32, name="lo_codes", align_bytes=64)
         lo_scales = keep.tile([P, NQ], U8, name="lo_scales", align_bytes=64)
         quantize(lo_codes, lo_scales, lo, slice(0, NQ))
-        hi_made = keep.tile([P, NQ], U32, name="hi_made", align_bytes=64)
-        hi_scales = keep.tile([P, NQ], U8, name="hi_scales", align_bytes=64)
-        quantize(hi_made, hi_scales, hi, slice(0, NQ))
+        hi_codes = keep.tile([P, NQ], U32, name="hi_codes", align_bytes=64)
+        hi_made = keep.tile([P, NQ], U8, name="hi_made", align_bytes=64)
+        nc.vector.memset(hi_made[:].bitcast(I32), 0)
+        quantize(hi_codes, hi_made, hi, slice(0, NQ))
 
         k_grouped = keep.tile([P, N, PACK], BF16, name="k_grouped", align_bytes=64)
         c_grouped = keep.tile([P, N, PACK], BF16, name="c_grouped", align_bytes=64)
@@ -104,10 +106,10 @@ def tile_attend_quest_f_topk_kernel(tc, qT, kT, cT, offs, out):
         nc.scalar.activation(c_grouped[:, halves[1], 2], c2_half[:].indirect(parts[1]), COPY)
         nc.vector.tensor_copy(c_grouped[:, :, 1], c_raw[1][:, :].indirect(offsets[:]))
         nc.vector.tensor_copy(c_grouped[:, :, 0], c_raw[0][:, :].indirect(offsets[:]))
-        hi_codes = keep.tile([P, NQ], U32, name="hi_codes", tag="c_raw1", align_bytes=64)
-        nc.gpsimd.tensor_copy(hi_codes[:], hi_made[:])
+        hi_scales = keep.tile([P, NQ], U8, name="hi_scales", tag="c_raw1", align_bytes=64)
+        nc.gpsimd.tensor_copy(hi_scales[:].bitcast(I32), hi_made[:].bitcast(I32))
         spare = psum.tile([P, N], F32, name="spare")
-        for repeat in range(3):
+        for repeat in range(4):
             nc.tensor.matmul_mx(
                 out=spare[0:32, :],
                 lhsT=hi_codes[:, 0:32].bitcast(FP8X4),

@@ -109,16 +109,15 @@ def tile_attend_quest_f_topk_kernel(tc, qT, kT, cT, offs, out):
         hi_scales = keep.tile([P, NQ], U8, name="hi_scales", tag="c_raw1", align_bytes=64)
         nc.gpsimd.tensor_copy(hi_scales[:].bitcast(I32), hi_made[:].bitcast(I32))
         spare = psum.tile([P, N], F32, name="spare")
-        for repeat in range(4):
-            nc.tensor.matmul_mx(
-                out=spare[0:32, :],
-                lhsT=hi_codes[:, 0:32].bitcast(FP8X4),
-                lhsT_scale=hi_scales[:, 0:32],
-                rhs=k_codes[:].bitcast(FP8X4),
-                rhs_scale=k_scales[:],
-                start=True,
-                stop=True,
-            )
+        nc.tensor.matmul_mx(
+            out=spare[:],
+            lhsT=hi_codes[:, q_tiles[0]].bitcast(FP8X4),
+            lhsT_scale=hi_scales[:, q_tiles[0]],
+            rhs=k_codes[:].bitcast(FP8X4),
+            rhs_scale=k_scales[:],
+            start=True,
+            stop=True,
+        )
         for g in range(len(groups)):
             multiply(g, hi_codes, hi_scales, k_codes, k_scales, True, False)
         nc.scalar.activation(c3_half[:, 0:768], c_raw[3][:, 0:768], COPY)

@@ -38,7 +38,7 @@ def tile_attend_quest_f_topk_kernel(tc, qT, kT, cT, offs, out):
         nc.sync.dma_start(offsets[:], offs)
         nc.sync.dma_start(out=k_raw[:, 0:2, :], in_=k_rows[:, 0:2, :])
         nc.sync.dma_start(out=k_raw[:, 2:4, :], in_=k_rows[:, 2:4, :])
-        for t in (2, 1, 0):
+        for t in (1, 2, 0):
             nc.sync.dma_start(out=c_raw[t][:, :], in_=c_rows[:, t, :])
         for cols in chunks:
             nc.sync.dma_start(out=c_raw[3][:, cols], in_=c_rows[:, 3, cols])
@@ -101,12 +101,12 @@ def tile_attend_quest_f_topk_kernel(tc, qT, kT, cT, offs, out):
 
         c2_half = keep.tile([P, T], BF16, name="c2_half")
         c3_half = keep.tile([P, T], BF16, name="c3_half")
+        nc.vector.tensor_copy(c_grouped[:, :, 1], c_raw[1][:, :].indirect(offsets[:]))
         nc.vector.tensor_copy(c_grouped[:, halves[0], 2], c_raw[2][:, :].indirect(parts[0]))
         nc.scalar.activation(c2_half[:], c_raw[2][:, :], COPY)
         nc.scalar.activation(c_grouped[:, halves[1], 2], c2_half[:].indirect(parts[1]), COPY)
-        nc.vector.tensor_copy(c_grouped[:, :, 1], c_raw[1][:, :].indirect(offsets[:]))
         nc.vector.tensor_copy(c_grouped[:, :, 0], c_raw[0][:, :].indirect(offsets[:]))
-        hi_scales = keep.tile([P, NQ], U8, name="hi_scales", tag="c_raw1", align_bytes=64)
+        hi_scales = keep.tile([P, NQ], U8, name="hi_scales", tag="c_raw2", align_bytes=64)
         nc.gpsimd.tensor_copy(hi_scales[:].bitcast(I32), hi_made[:].bitcast(I32))
         spare = psum.tile([P, N], F32, name="spare")
         nc.tensor.matmul_mx(

@@ -34,7 +34,7 @@ def tile_attend_quest_f_topk_kernel(tc, qT, kT, cT, offs, out):
         c_rows = cT.rearrange("(p t) w -> p t w", t=PACK)
         chunks = [slice(0, 1088), slice(1088, 1792), slice(1792, 2048)]
 
-        nc.sync.dma_start(out=q_raw[:], in_=qT[0].rearrange("(p t) w -> p t w", t=PACK))
+        nc.scalar.dma_start(out=q_raw[:], in_=qT[0].rearrange("(p t) w -> p t w", t=PACK))
         nc.sync.dma_start(offsets[:], offs)
         nc.sync.dma_start(out=k_raw[:, 0:2, :], in_=k_rows[:, 0:2, :])
         nc.sync.dma_start(out=k_raw[:, 2:4, :], in_=k_rows[:, 2:4, :])

@@ -8,7 +8,6 @@ FLOPS = 2 * 2 * NQ * D * N
 F32 = mybir.dt.float32
 BF16 = mybir.dt.bfloat16
 U32 = mybir.dt.uint32
-I32 = mybir.dt.int32
 U16 = mybir.dt.uint16
 U8 = mybir.dt.uint8
 FP8X4 = mybir.dt.float8_e4m3fn_x4
@@ -29,19 +28,17 @@ def tile_attend_quest_f_topk_kernel(tc, qT, kT, cT, offs, out):
         offsets = keep.tile([P, N // 16], U16, name="offsets")
         q_raw = keep.tile([P, PACK, NQ], F32, name="q_raw")
         k_raw = keep.tile([P, PACK, T], F32, name="k_raw")
-        c_raw = [keep.tile([P, T], F32, name="c_raw%d" % t, tag="c_raw%d" % t, align_bytes=64) for t in range(PACK)]
-        k_rows = kT.rearrange("(p t) w -> p t w", t=PACK)
+        c01_raw = keep.tile([P, 2, T], F32, name="c01_raw")
+        c2_raw = keep.tile([P, T], F32, name="c2_raw")
+        c3_raw = keep.tile([P, T], F32, name="c3_raw", tag="c3_raw", align_bytes=64)
         c_rows = cT.rearrange("(p t) w -> p t w", t=PACK)
-        chunks = [slice(0, 1088), slice(1088, 1792), slice(1792, 2048)]
 
         nc.scalar.dma_start(out=q_raw[:], in_=qT[0].rearrange("(p t) w -> p t w", t=PACK))
         nc.sync.dma_start(offsets[:], offs)
-        nc.sync.dma_start(out=k_raw[:, 0:2, :], in_=k_rows[:, 0:2, :])
-        nc.sync.dma_start(out=k_raw[:, 2:4, :], in_=k_rows[:, 2:4, :])
-        for t in (1, 2, 0):
-            nc.sync.dma_start(out=c_raw[t][:, :], in_=c_rows[:, t, :])
-        for cols in chunks:
-            nc.sync.dma_start(out=c_raw[3][:, cols], in_=c_rows[:, 3, cols])
+        nc.sync.dma_start(out=k_raw[:], in_=kT.rearrange("(p t) w -> p t w", t=PACK))
+        nc.sync.dma_start(out=c01_raw[:], in_=c_rows[:, 0:2, :])
+        nc.sync.dma_start(out=c2_raw[:], in_=c_rows[:, 2, :])
+        nc.sync.dma_start(out=c3_raw[:], in_=c_rows[:, 3, :])
 
         def quantize(codes, scales, grouped, cols):
             nc.vector.quantize_mx(
@@ -49,6 +46,13 @@ def tile_attend_quest_f_topk_kernel(tc, qT, kT, cT, offs, out):
                 scales=scales[:, cols],
                 in_=grouped[:, cols, :].rearrange("p w t -> p (w t)"),
             )
+
+        def listed(cols):
+            return offsets[:, cols.start // 16 : cols.stop // 16]
+
+        halves = [slice(0, HALF), slice(HALF, N)]
+        quarters = [slice(h * P, (h + 1) * P) for h in range(N // P)]
+        q_tiles = [slice(m * P, (m + 1) * P) for m in range(2)]
 
         q_view = q_raw[:].rearrange("p t w -> p w t")
         hi = keep.tile([P, NQ, PACK], BF16, name="hi", align_bytes=64)
@@ -59,21 +63,45 @@ def tile_attend_quest_f_topk_kernel(tc, qT, kT, cT, offs, out):
         lo_scales = keep.tile([P, NQ], U8, name="lo_scales", align_bytes=64)
         quantize(lo_codes, lo_scales, lo, slice(0, NQ))
         hi_codes = keep.tile([P, NQ], U32, name="hi_codes", align_bytes=64)
-        hi_made = keep.tile([P, NQ], U8, name="hi_made", align_bytes=64)
-        nc.vector.memset(hi_made[:].bitcast(I32), 0)
-        quantize(hi_codes, hi_made, hi, slice(0, NQ))
+        hi_scales = keep.tile([P, NQ], U8, name="hi_scales", align_bytes=64)
+        quantize(hi_codes, hi_scales, hi, slice(0, NQ))
 
         k_grouped = keep.tile([P, N, PACK], BF16, name="k_grouped", align_bytes=64)
         c_grouped = keep.tile([P, N, PACK], BF16, name="c_grouped", align_bytes=64)
-        k_codes = keep.tile([P, N], U32, name="k_codes", align_bytes=64)
         k_scales = keep.tile([P, N], U8, name="k_scales", align_bytes=64)
-        c_codes = keep.tile([P, N], U32, name="c_codes", align_bytes=64)
         c_scales = keep.tile([P, N], U8, name="c_scales", align_bytes=64)
 
-        halves = [slice(0, HALF), slice(HALF, N)]
-        quarters = [slice(h * P, (h + 1) * P) for h in range(N // P)]
-        q_tiles = [slice(m * P, (m + 1) * P) for m in range(2)]
-        groups = [(0, quarters[0]), (0, quarters[1]), (1, halves[0])] + [(m, cols) for cols in quarters[2:] for m in range(2)]
+        k_picked = keep.tile([P, PACK, HALF], F32, name="k_picked")
+        for t in range(PACK):
+            nc.vector.tensor_copy(k_grouped[:, halves[0], t], k_raw[:, t, :].indirect(listed(halves[0])))
+            nc.scalar.activation(k_picked[:, t, :], k_raw[:, t, :].indirect(listed(halves[1])), COPY)
+        nc.scalar.activation(
+            k_grouped[:, halves[1], :].rearrange("p (c i) t -> p c t i", i=4),
+            k_picked[:].rearrange("p t (c i) -> p c t i", i=4),
+            COPY,
+        )
+
+        c01_picked = keep.tile([P, 2, HALF], F32, name="c01_picked", tag="c01_picked", align_bytes=64)
+        for t in range(2):
+            nc.vector.tensor_copy(c_grouped[:, halves[0], t], c01_raw[:, t, :].indirect(listed(halves[0])))
+            nc.scalar.activation(c01_picked[:, t, :], c01_raw[:, t, :].indirect(listed(halves[1])), COPY)
+        nc.scalar.activation(c_grouped[:, halves[1], 0:2], c01_picked[:].rearrange("p t n -> p n t"), COPY)
+
+        k_codes = keep.tile([P, N], U32, name="k_codes", tag="c01_picked", align_bytes=64)
+        quantize(k_codes, k_scales, k_grouped, slice(0, N))
+
+        def gather_plane(raw, t):
+            picked = [keep.tile([P, P], BF16, name="picked%d_%d" % (t, h)) for h in range(2)]
+            nc.vector.tensor_copy(c_grouped[:, halves[0], t], raw[:].indirect(listed(halves[0])))
+            for h in range(2):
+                nc.scalar.activation(picked[h][:], raw[:].indirect(listed(quarters[2 + h])), COPY)
+            nc.vector.tensor_copy(c_grouped[:, quarters[2], t], picked[0][:])
+            nc.scalar.activation(c_grouped[:, quarters[3], t], picked[1][:], COPY)
+
+        gather_plane(c2_raw, 2)
+
+        groups = [(m, cols) for cols in quarters for m in range(2)]
+        stores = {1: quarters[0], 3: quarters[1], 7: halves[1]}
         banks = [psum.tile([P, cols.stop - cols.start], F32, name="bank%d" % g) for g, (m, cols) in enumerate(groups)]
 
         def multiply(g, q_codes, q_scales, codes, scales, start, stop):
@@ -88,56 +116,21 @@ def tile_attend_quest_f_topk_kernel(tc, qT, kT, cT, offs, out):
                 stop=stop,
             )
 
-        parts = [offsets[:, h * HALF // 16 : (h + 1) * HALF // 16] for h in range(2)]
-        for t in range(2):
-            nc.vector.tensor_copy(k_grouped[:, :, t], k_raw[:, t, :].indirect(offsets[:]))
-        picked = keep.tile([P, 2, HALF], F32, name="picked")
-        for t in range(2):
-            nc.vector.tensor_copy(picked[:, t, :], k_raw[:, 2 + t, :].indirect(parts[1]))
-        nc.scalar.activation(k_grouped[:, halves[1], 2:4], picked[:].rearrange("p t n -> p n t"), COPY)
-        for t in range(2, PACK):
-            nc.vector.tensor_copy(k_grouped[:, halves[0], t], k_raw[:, t, :].indirect(parts[0]))
-        quantize(k_codes, k_scales, k_grouped, slice(0, N))
-
-        c2_half = keep.tile([P, T], BF16, name="c2_half")
-        c3_half = keep.tile([P, T], BF16, name="c3_half")
-        nc.vector.tensor_copy(c_grouped[:, :, 1], c_raw[1][:, :].indirect(offsets[:]))
-        nc.vector.tensor_copy(c_grouped[:, halves[0], 2], c_raw[2][:, :].indirect(parts[0]))
-        nc.scalar.activation(c2_half[:], c_raw[2][:, :], COPY)
-        nc.scalar.activation(c_grouped[:, halves[1], 2], c2_half[:].indirect(parts[1]), COPY)
-        nc.vector.tensor_copy(c_grouped[:, :, 0], c_raw[0][:, :].indirect(offsets[:]))
-        hi_scales = keep.tile([P, NQ], U8, name="hi_scales", tag="c_raw2", align_bytes=64)
-        nc.gpsimd.tensor_copy(hi_scales[:].bitcast(I32), hi_made[:].bitcast(I32))
-        spare = psum.tile([P, N], F32, name="spare")
-        nc.tensor.matmul_mx(
-            out=spare[:],
-            lhsT=hi_codes[:, q_tiles[0]].bitcast(FP8X4),
-            lhsT_scale=hi_scales[:, q_tiles[0]],
-            rhs=k_codes[:].bitcast(FP8X4),
-            rhs_scale=k_scales[:],
-            start=True,
-            stop=True,
-        )
         for g in range(len(groups)):
             multiply(g, hi_codes, hi_scales, k_codes, k_scales, True, False)
-        nc.scalar.activation(c3_half[:, 0:768], c_raw[3][:, 0:768], COPY)
-        nc.vector.tensor_copy(c3_half[:, 768:1088], c_raw[3][:, 768:1088])
-        nc.scalar.activation(c3_half[:, 1088:1344], c_raw[3][:, 1088:1344], COPY)
-        nc.vector.tensor_copy(c3_half[:, 1344:1792], c_raw[3][:, 1344:1792])
-        nc.scalar.activation(c3_half[:, 1792:2048], c_raw[3][:, 1792:2048], COPY)
-        nc.vector.tensor_copy(c_grouped[:, halves[0], 3], c_raw[3][:, :].indirect(parts[0]))
-        nc.scalar.activation(c_grouped[:, halves[1], 3], c3_half[:].indirect(parts[1]), COPY)
+
+        gather_plane(c3_raw, 3)
+        c_codes = keep.tile([P, N], U32, name="c_codes", tag="c3_raw", align_bytes=64)
         for cols in quarters:
             quantize(c_codes, c_scales, c_grouped, cols)
-        results = [keep.tile([P, N], F32, name="result%d" % m) for m in range(2)]
+
+        result = keep.tile([P, 2, N], F32, name="result")
+        out_rows = out[0].rearrange("(m p) n -> p m n", p=P)
         for g, (m, cols) in enumerate(groups):
             multiply(g, lo_codes, lo_scales, c_codes, c_scales, False, True)
-            if m == 0 and cols.start >= HALF:
-                nc.vector.tensor_copy(results[m][:, cols], banks[g][:])
+            if m == 0:
+                nc.scalar.copy(result[:, m, cols], banks[g][:])
             else:
-                nc.scalar.copy(results[m][:, cols], banks[g][:])
-            if g < 2:
-                nc.sync.dma_start(out=out[0, q_tiles[m], cols], in_=results[m][:, cols])
-            elif cols.stop % HALF == 0:
-                half = halves[cols.start // HALF]
-                nc.sync.dma_start(out=out[0, q_tiles[m], half], in_=results[m][:, half])
+                nc.vector.tensor_copy(result[:, m, cols], banks[g][:])
+            if g in stores:
+                nc.sync.dma_start(out=out_rows[:, :, stores[g]], in_=result[:, :, stores[g]])

@@ -28,7 +28,7 @@ def tile_attend_quest_f_topk_kernel(tc, qT, kT, cT, offs, out):
         offsets = keep.tile([P, N // 16], U16, name="offsets")
         q_raw = keep.tile([P, PACK, NQ], F32, name="q_raw")
         k_raw = keep.tile([P, PACK, T], F32, name="k_raw")
-        c01_raw = keep.tile([P, 2, T], F32, name="c01_raw")
+        c01_raw = keep.tile([P, 2, T], F32, name="c01_raw", tag="c01_raw", align_bytes=64)
         c2_raw = keep.tile([P, T], F32, name="c2_raw")
         c3_raw = keep.tile([P, T], F32, name="c3_raw", tag="c3_raw", align_bytes=64)
         c_rows = cT.rearrange("(p t) w -> p t w", t=PACK)
@@ -62,15 +62,9 @@ def tile_attend_quest_f_topk_kernel(tc, qT, kT, cT, offs, out):
         lo_codes = keep.tile([P, NQ], U32, name="lo_codes", align_bytes=64)
         lo_scales = keep.tile([P, NQ], U8, name="lo_scales", align_bytes=64)
         quantize(lo_codes, lo_scales, lo, slice(0, NQ))
-        hi_codes = keep.tile([P, NQ], U32, name="hi_codes", align_bytes=64)
-        hi_scales = keep.tile([P, NQ], U8, name="hi_scales", align_bytes=64)
-        quantize(hi_codes, hi_scales, hi, slice(0, NQ))
 
         k_grouped = keep.tile([P, N, PACK], BF16, name="k_grouped", align_bytes=64)
         c_grouped = keep.tile([P, N, PACK], BF16, name="c_grouped", align_bytes=64)
-        k_scales = keep.tile([P, N], U8, name="k_scales", align_bytes=64)
-        c_scales = keep.tile([P, N], U8, name="c_scales", align_bytes=64)
-
         k_picked = keep.tile([P, PACK, HALF], F32, name="k_picked")
         for t in range(PACK):
             nc.vector.tensor_copy(k_grouped[:, halves[0], t], k_raw[:, t, :].indirect(listed(halves[0])))
@@ -81,24 +75,21 @@ def tile_attend_quest_f_topk_kernel(tc, qT, kT, cT, offs, out):
             COPY,
         )
 
-        c01_picked = keep.tile([P, 2, HALF], F32, name="c01_picked", tag="c01_picked", align_bytes=64)
-        for t in range(2):
-            nc.vector.tensor_copy(c_grouped[:, halves[0], t], c01_raw[:, t, :].indirect(listed(halves[0])))
-            nc.scalar.activation(c01_picked[:, t, :], c01_raw[:, t, :].indirect(listed(halves[1])), COPY)
-        nc.scalar.activation(c_grouped[:, halves[1], 0:2], c01_picked[:].rearrange("p t n -> p n t"), COPY)
-
-        k_codes = keep.tile([P, N], U32, name="k_codes", tag="c01_picked", align_bytes=64)
-        quantize(k_codes, k_scales, k_grouped, slice(0, N))
-
-        def gather_plane(raw, t):
-            picked = [keep.tile([P, P], BF16, name="picked%d_%d" % (t, h)) for h in range(2)]
-            nc.vector.tensor_copy(c_grouped[:, halves[0], t], raw[:].indirect(listed(halves[0])))
+        early = [keep.tile([P, 3, P], F32, name="early%d" % h) for h in range(2)]
+        for t, window in enumerate([c01_raw[:, 0, :], c01_raw[:, 1, :], c2_raw[:]]):
+            nc.vector.tensor_copy(c_grouped[:, halves[0], t], window.indirect(listed(halves[0])))
             for h in range(2):
-                nc.scalar.activation(picked[h][:], raw[:].indirect(listed(quarters[2 + h])), COPY)
-            nc.vector.tensor_copy(c_grouped[:, quarters[2], t], picked[0][:])
-            nc.scalar.activation(c_grouped[:, quarters[3], t], picked[1][:], COPY)
+                nc.scalar.activation(early[h][:, t, :], window.indirect(listed(quarters[2 + h])), COPY)
+        nc.vector.tensor_copy(c_grouped[:, quarters[2], 0:3], early[0][:].rearrange("p t n -> p n t"))
+        nc.scalar.activation(c_grouped[:, quarters[3], 0:3], early[1][:].rearrange("p t n -> p n t"), COPY)
 
-        gather_plane(c2_raw, 2)
+        first_codes = keep.tile([P, N + NQ], U32, name="first_codes", tag="c01_raw", align_bytes=64)
+        k_codes = first_codes[:, 0:N]
+        hi_codes = first_codes[:, N : N + NQ]
+        k_scales = keep.tile([P, N], U8, name="k_scales", align_bytes=64)
+        hi_scales = keep.tile([P, NQ], U8, name="hi_scales", align_bytes=64)
+        quantize(k_codes, k_scales, k_grouped, slice(0, N))
+        quantize(hi_codes, hi_scales, hi, slice(0, NQ))
 
         groups = [(m, cols) for cols in quarters for m in range(2)]
         stores = {1: quarters[0], 3: quarters[1], 7: halves[1]}
@@ -119,8 +110,14 @@ def tile_attend_quest_f_topk_kernel(tc, qT, kT, cT, offs, out):
         for g in range(len(groups)):
             multiply(g, hi_codes, hi_scales, k_codes, k_scales, True, False)
 
-        gather_plane(c3_raw, 3)
+        last = [keep.tile([P, P], BF16, name="last%d" % h) for h in range(2)]
+        nc.vector.tensor_copy(c_grouped[:, halves[0], 3], c3_raw[:].indirect(listed(halves[0])))
+        for h in range(2):
+            nc.scalar.activation(last[h][:], c3_raw[:].indirect(listed(quarters[2 + h])), COPY)
+        nc.vector.tensor_copy(c_grouped[:, quarters[2], 3], last[0][:])
+        nc.scalar.activation(c_grouped[:, quarters[3], 3], last[1][:], COPY)
         c_codes = keep.tile([P, N], U32, name="c_codes", tag="c3_raw", align_bytes=64)
+        c_scales = keep.tile([P, N], U8, name="c_scales", align_bytes=64)
         for cols in quarters:
             quantize(c_codes, c_scales, c_grouped, cols)
 

@@ -17,6 +17,7 @@ COPY = mybir.ActivationFunctionType.Copy
 P = 128
 PACK = 4
 HALF = N // 2
+WARM_ROWS = 32
 
 
 def tile_attend_quest_f_topk_kernel(tc, qT, kT, cT, offs, out):
@@ -93,12 +94,12 @@ def tile_attend_quest_f_topk_kernel(tc, qT, kT, cT, offs, out):
 
         groups = [(m, cols) for cols in quarters for m in range(2)]
         stores = {1: quarters[0], 3: quarters[1], 7: halves[1]}
-        banks = [psum.tile([P, cols.stop - cols.start], F32, name="bank%d" % g) for g, (m, cols) in enumerate(groups)]
+        banks = [psum.tile([P, N], F32, name="bank%d" % g) for g in range(len(groups))]
 
         def multiply(g, q_codes, q_scales, codes, scales, start, stop):
             m, cols = groups[g]
             nc.tensor.matmul_mx(
-                out=banks[g][:],
+                out=banks[g][:, 0:P],
                 lhsT=q_codes[:, q_tiles[m]].bitcast(FP8X4),
                 lhsT_scale=q_scales[:, q_tiles[m]],
                 rhs=codes[:, cols].bitcast(FP8X4),
@@ -107,6 +108,15 @@ def tile_attend_quest_f_topk_kernel(tc, qT, kT, cT, offs, out):
                 stop=stop,
             )
 
+        nc.tensor.matmul_mx(
+            out=banks[-1][0:WARM_ROWS, :],
+            lhsT=hi_codes[:, 0:WARM_ROWS].bitcast(FP8X4),
+            lhsT_scale=hi_scales[:, 0:WARM_ROWS],
+            rhs=k_codes[:, 0:N].bitcast(FP8X4),
+            rhs_scale=k_scales[:],
+            start=True,
+            stop=True,
+        )
         for g in range(len(groups)):
             multiply(g, hi_codes, hi_scales, k_codes, k_scales, True, False)
 
@@ -126,8 +136,8 @@ def tile_attend_quest_f_topk_kernel(tc, qT, kT, cT, offs, out):
         for g, (m, cols) in enumerate(groups):
             multiply(g, lo_codes, lo_scales, c_codes, c_scales, False, True)
             if m == 0:
-                nc.scalar.copy(result[:, m, cols], banks[g][:])
+                nc.scalar.copy(result[:, m, cols], banks[g][:, 0:P])
             else:
-                nc.vector.tensor_copy(result[:, m, cols], banks[g][:])
+                nc.vector.tensor_copy(result[:, m, cols], banks[g][:, 0:P])
             if g in stores:
                 nc.sync.dma_start(out=out_rows[:, :, stores[g]], in_=result[:, :, stores[g]])

@@ -93,7 +93,7 @@ def tile_attend_quest_f_topk_kernel(tc, qT, kT, cT, offs, out):
         quantize(hi_codes, hi_scales, hi, slice(0, NQ))
 
         groups = [(m, cols) for cols in quarters for m in range(2)]
-        stores = {1: quarters[0], 3: quarters[1], 7: halves[1]}
+        stores = {0: (slice(0, 1), quarters[0]), 1: (slice(1, 2), quarters[0]), 3: (slice(0, 2), quarters[1]), 5: (slice(0, 2), quarters[2]), 7: (slice(0, 2), quarters[3])}
         banks = [psum.tile([P, N], F32, name="bank%d" % g) for g in range(len(groups))]
 
         def multiply(g, q_codes, q_scales, codes, scales, start, stop):
@@ -135,9 +135,10 @@ def tile_attend_quest_f_topk_kernel(tc, qT, kT, cT, offs, out):
         out_rows = out[0].rearrange("(m p) n -> p m n", p=P)
         for g, (m, cols) in enumerate(groups):
             multiply(g, lo_codes, lo_scales, c_codes, c_scales, False, True)
-            if m == 0:
+            if g in (0, 1, 4, 6):
                 nc.scalar.copy(result[:, m, cols], banks[g][:, 0:P])
             else:
                 nc.vector.tensor_copy(result[:, m, cols], banks[g][:, 0:P])
             if g in stores:
-                nc.sync.dma_start(out=out_rows[:, :, stores[g]], in_=result[:, :, stores[g]])
+                tiles, slots = stores[g]
+                nc.sync.dma_start(out=out_rows[:, tiles, slots], in_=result[:, tiles, slots])

@@ -92,8 +92,8 @@ def tile_attend_quest_f_topk_kernel(tc, qT, kT, cT, offs, out):
         quantize(k_codes, k_scales, k_grouped, slice(0, N))
         quantize(hi_codes, hi_scales, hi, slice(0, NQ))
 
-        groups = [(m, cols) for cols in quarters for m in range(2)]
-        stores = {0: (slice(0, 1), quarters[0]), 1: (slice(1, 2), quarters[0]), 3: (slice(0, 2), quarters[1]), 5: (slice(0, 2), quarters[2]), 7: (slice(0, 2), quarters[3])}
+        groups = [(m, quarters[h]) for m, h in [(0, 0), (1, 0), (1, 1), (0, 1), (0, 2), (0, 3), (1, 2), (1, 3)]]
+        stores = {0: quarters[0], 2: halves[0], 5: slice(P, N), 7: halves[1]}
         banks = [psum.tile([P, N], F32, name="bank%d" % g) for g in range(len(groups))]
 
         def multiply(g, q_codes, q_scales, codes, scales, start, stop):
@@ -135,10 +135,9 @@ def tile_attend_quest_f_topk_kernel(tc, qT, kT, cT, offs, out):
         out_rows = out[0].rearrange("(m p) n -> p m n", p=P)
         for g, (m, cols) in enumerate(groups):
             multiply(g, lo_codes, lo_scales, c_codes, c_scales, False, True)
-            if g in (0, 1, 4, 6):
+            if g in (0, 1, 4, 5):
                 nc.scalar.copy(result[:, m, cols], banks[g][:, 0:P])
             else:
                 nc.vector.tensor_copy(result[:, m, cols], banks[g][:, 0:P])
             if g in stores:
-                tiles, slots = stores[g]
-                nc.sync.dma_start(out=out_rows[:, tiles, slots], in_=result[:, tiles, slots])
+                nc.sync.dma_start(out=out_rows[:, m, stores[g]], in_=result[:, m, stores[g]])

@@ -120,12 +120,14 @@ def tile_attend_quest_f_topk_kernel(tc, qT, kT, cT, offs, out):
         for g in range(len(groups)):
             multiply(g, hi_codes, hi_scales, k_codes, k_scales, True, False)
 
-        last = [keep.tile([P, P], BF16, name="last%d" % h) for h in range(2)]
+        pieces = [slice(3 * P, 3 * P + P // 2), quarters[2], slice(3 * P + P // 2, N)]
+        last = [keep.tile([P, cols.stop - cols.start], BF16, name="last%d" % h) for h, cols in enumerate(pieces)]
         nc.vector.tensor_copy(c_grouped[:, halves[0], 3], c3_raw[:].indirect(listed(halves[0])))
-        for h in range(2):
-            nc.scalar.activation(last[h][:], c3_raw[:].indirect(listed(quarters[2 + h])), COPY)
-        nc.vector.tensor_copy(c_grouped[:, quarters[2], 3], last[0][:])
-        nc.scalar.activation(c_grouped[:, quarters[3], 3], last[1][:], COPY)
+        for h, cols in enumerate(pieces):
+            nc.scalar.activation(last[h][:], c3_raw[:].indirect(listed(cols)), COPY)
+        nc.vector.tensor_copy(c_grouped[:, pieces[1], 3], last[1][:])
+        for h in (0, 2):
+            nc.scalar.activation(c_grouped[:, pieces[h], 3], last[h][:], COPY)
         c_codes = keep.tile([P, N], U32, name="c_codes", tag="c3_raw", align_bytes=64)
         c_scales = keep.tile([P, N], U8, name="c_scales", align_bytes=64)
         for cols in quarters:

@@ -18,6 +18,7 @@ P = 128
 PACK = 4
 HALF = N // 2
 WARM_ROWS = 32
+DMA_ALIGN = 512
 
 
 def tile_attend_quest_f_topk_kernel(tc, qT, kT, cT, offs, out):
@@ -27,11 +28,11 @@ def tile_attend_quest_f_topk_kernel(tc, qT, kT, cT, offs, out):
         psum = ctx.enter_context(tc.psum_pool(name="psum", bufs=1))
 
         offsets = keep.tile([P, N // 16], U16, name="offsets")
-        q_raw = keep.tile([P, PACK, NQ], F32, name="q_raw")
-        k_raw = keep.tile([P, PACK, T], F32, name="k_raw")
-        c01_raw = keep.tile([P, 2, T], F32, name="c01_raw", tag="c01_raw", align_bytes=64)
-        c2_raw = keep.tile([P, T], F32, name="c2_raw")
-        c3_raw = keep.tile([P, T], F32, name="c3_raw", tag="c3_raw", align_bytes=64)
+        q_raw = keep.tile([P, PACK, NQ], F32, name="q_raw", align_bytes=DMA_ALIGN)
+        k_raw = keep.tile([P, PACK, T], F32, name="k_raw", align_bytes=DMA_ALIGN)
+        c01_raw = keep.tile([P, 2, T], F32, name="c01_raw", tag="c01_raw", align_bytes=DMA_ALIGN)
+        c2_raw = keep.tile([P, T], F32, name="c2_raw", align_bytes=DMA_ALIGN)
+        c3_raw = keep.tile([P, T], F32, name="c3_raw", tag="c3_raw", align_bytes=DMA_ALIGN)
         c_rows = cT.rearrange("(p t) w -> p t w", t=PACK)
 
         nc.scalar.dma_start(out=q_raw[:], in_=qT[0].rearrange("(p t) w -> p t w", t=PACK))
@@ -84,7 +85,7 @@ def tile_attend_quest_f_topk_kernel(tc, qT, kT, cT, offs, out):
         nc.vector.tensor_copy(c_grouped[:, quarters[2], 0:3], early[0][:].rearrange("p t n -> p n t"))
         nc.scalar.activation(c_grouped[:, quarters[3], 0:3], early[1][:].rearrange("p t n -> p n t"), COPY)
 
-        first_codes = keep.tile([P, N + NQ], U32, name="first_codes", tag="c01_raw", align_bytes=64)
+        first_codes = keep.tile([P, N + NQ], U32, name="first_codes", tag="c01_raw", align_bytes=DMA_ALIGN)
         k_codes = first_codes[:, 0:N]
         hi_codes = first_codes[:, N : N + NQ]
         k_scales = keep.tile([P, N], U8, name="k_scales", align_bytes=64)
@@ -128,12 +129,12 @@ def tile_attend_quest_f_topk_kernel(tc, qT, kT, cT, offs, out):
         nc.vector.tensor_copy(c_grouped[:, pieces[1], 3], last[1][:])
         for h in (0, 2):
             nc.scalar.activation(c_grouped[:, pieces[h], 3], last[h][:], COPY)
-        c_codes = keep.tile([P, N], U32, name="c_codes", tag="c3_raw", align_bytes=64)
+        c_codes = keep.tile([P, N], U32, name="c_codes", tag="c3_raw", align_bytes=DMA_ALIGN)
         c_scales = keep.tile([P, N], U8, name="c_scales", align_bytes=64)
         for cols in quarters:
             quantize(c_codes, c_scales, c_grouped, cols)
 
-        result = keep.tile([P, 2, N], F32, name="result")
+        result = keep.tile([P, 2, N], F32, name="result", align_bytes=DMA_ALIGN)
         out_rows = out[0].rearrange("(m p) n -> p m n", p=P)
         for g, (m, cols) in enumerate(groups):
             multiply(g, lo_codes, lo_scales, c_codes, c_scales, False, True)

@@ -77,13 +77,16 @@ def tile_attend_quest_f_topk_kernel(tc, qT, kT, cT, offs, out):
             COPY,
         )
 
-        early = [keep.tile([P, 3, P], F32, name="early%d" % h) for h in range(2)]
+        early_v = keep.tile([P, 2, P], F32, name="early_v")
+        late_v = keep.tile([P, 2, P], BF16, name="late_v")
+        early_s = keep.tile([P, 3, P], F32, name="early_s")
         for t, window in enumerate([c01_raw[:, 0, :], c01_raw[:, 1, :], c2_raw[:]]):
             nc.vector.tensor_copy(c_grouped[:, halves[0], t], window.indirect(listed(halves[0])))
-            for h in range(2):
-                nc.scalar.activation(early[h][:, t, :], window.indirect(listed(quarters[2 + h])), COPY)
-        nc.vector.tensor_copy(c_grouped[:, quarters[2], 0:3], early[0][:].rearrange("p t n -> p n t"))
-        nc.scalar.activation(c_grouped[:, quarters[3], 0:3], early[1][:].rearrange("p t n -> p n t"), COPY)
+            staged = early_v[:, t, :] if t < 2 else late_v[:, 0, :]
+            nc.scalar.activation(staged, window.indirect(listed(quarters[2])), COPY)
+            nc.scalar.activation(early_s[:, t, :], window.indirect(listed(quarters[3])), COPY)
+        nc.vector.tensor_copy(c_grouped[:, quarters[2], 0:2], early_v[:].rearrange("p t n -> p n t"))
+        nc.scalar.activation(c_grouped[:, quarters[3], 0:3], early_s[:].rearrange("p t n -> p n t"), COPY)
 
         first_codes = keep.tile([P, N + NQ], U32, name="first_codes", tag="c01_raw", align_bytes=DMA_ALIGN)
         k_codes = first_codes[:, 0:N]
@@ -122,11 +125,11 @@ def tile_attend_quest_f_topk_kernel(tc, qT, kT, cT, offs, out):
             multiply(g, hi_codes, hi_scales, k_codes, k_scales, True, False)
 
         pieces = [slice(3 * P, 3 * P + P // 2), quarters[2], slice(3 * P + P // 2, N)]
-        last = [keep.tile([P, cols.stop - cols.start], BF16, name="last%d" % h) for h, cols in enumerate(pieces)]
+        last = {h: keep.tile([P, P // 2], BF16, name="last%d" % h) for h in (0, 2)}
         nc.vector.tensor_copy(c_grouped[:, halves[0], 3], c3_raw[:].indirect(listed(halves[0])))
-        for h, cols in enumerate(pieces):
-            nc.scalar.activation(last[h][:], c3_raw[:].indirect(listed(cols)), COPY)
-        nc.vector.tensor_copy(c_grouped[:, pieces[1], 3], last[1][:])
+        for staged, cols in zip([last[0][:], late_v[:, 1, :], last[2][:]], pieces):
+            nc.scalar.activation(staged, c3_raw[:].indirect(listed(cols)), COPY)
+        nc.vector.tensor_copy(c_grouped[:, pieces[1], 2:4], late_v[:].rearrange("p t n -> p n t"))
         for h in (0, 2):
             nc.scalar.activation(c_grouped[:, pieces[h], 3], last[h][:], COPY)
         c_codes = keep.tile([P, N], U32, name="c_codes", tag="c3_raw", align_bytes=DMA_ALIGN)

@@ -96,8 +96,8 @@ def tile_attend_quest_f_topk_kernel(tc, qT, kT, cT, offs, out):
         quantize(k_codes, k_scales, k_grouped, slice(0, N))
         quantize(hi_codes, hi_scales, hi, slice(0, NQ))
 
-        groups = [(m, quarters[h]) for m, h in [(0, 0), (1, 0), (1, 1), (0, 1), (0, 2), (0, 3), (1, 2), (1, 3)]]
-        stores = {0: quarters[0], 2: halves[0], 5: slice(P, N), 7: halves[1]}
+        groups = [(m, quarters[h]) for m, h in [(0, 0), (1, 0), (0, 1), (1, 1), (0, 2), (1, 2), (0, 3), (1, 3)]]
+        stores = {0: quarters[0], 2: quarters[1], 3: halves[0], 6: halves[1], 7: halves[1]}
         banks = [psum.tile([P, N], F32, name="bank%d" % g) for g in range(len(groups))]
 
         def multiply(g, q_codes, q_scales, codes, scales, start, stop):
@@ -141,7 +141,7 @@ def tile_attend_quest_f_topk_kernel(tc, qT, kT, cT, offs, out):
         out_rows = out[0].rearrange("(m p) n -> p m n", p=P)
         for g, (m, cols) in enumerate(groups):
             multiply(g, lo_codes, lo_scales, c_codes, c_scales, False, True)
-            if g in (0, 1, 4, 5):
+            if m == 0:
                 nc.scalar.copy(result[:, m, cols], banks[g][:, 0:P])
             else:
                 nc.vector.tensor_copy(result[:, m, cols], banks[g][:, 0:P])

@@ -54,6 +54,7 @@ def tile_attend_quest_f_topk_kernel(tc, qT, kT, cT, offs, out):
 
         halves = [slice(0, HALF), slice(HALF, N)]
         quarters = [slice(h * P, (h + 1) * P) for h in range(N // P)]
+        middle = slice(P, 3 * P)
         q_tiles = [slice(m * P, (m + 1) * P) for m in range(2)]
 
         q_view = q_raw[:].rearrange("p t w -> p w t")
@@ -77,16 +78,16 @@ def tile_attend_quest_f_topk_kernel(tc, qT, kT, cT, offs, out):
             COPY,
         )
 
-        early_v = keep.tile([P, 2, P], F32, name="early_v")
-        late_v = keep.tile([P, 2, P], BF16, name="late_v")
-        early_s = keep.tile([P, 3, P], F32, name="early_s")
-        for t, window in enumerate([c01_raw[:, 0, :], c01_raw[:, 1, :], c2_raw[:]]):
-            nc.vector.tensor_copy(c_grouped[:, halves[0], t], window.indirect(listed(halves[0])))
-            staged = early_v[:, t, :] if t < 2 else late_v[:, 0, :]
-            nc.scalar.activation(staged, window.indirect(listed(quarters[2])), COPY)
-            nc.scalar.activation(early_s[:, t, :], window.indirect(listed(quarters[3])), COPY)
-        nc.vector.tensor_copy(c_grouped[:, quarters[2], 0:2], early_v[:].rearrange("p t n -> p n t"))
-        nc.scalar.activation(c_grouped[:, quarters[3], 0:3], early_s[:].rearrange("p t n -> p n t"), COPY)
+        c_picked = keep.tile([P, 2, HALF], F32, name="c_picked")
+        for t in range(2):
+            nc.vector.tensor_copy(c_grouped[:, halves[0], t], c01_raw[:, t, :].indirect(listed(halves[0])))
+            nc.scalar.activation(c_picked[:, t, :], c01_raw[:, t, :].indirect(listed(halves[1])), COPY)
+        nc.scalar.activation(c_grouped[:, halves[1], 0:2], c_picked[:].rearrange("p t n -> p n t"), COPY)
+
+        def gather_plane(t, window):
+            nc.vector.tensor_copy(c_grouped[:, middle, t], window[:].indirect(listed(middle)))
+            for cols in (quarters[0], quarters[3]):
+                nc.scalar.activation(c_grouped[:, cols, t], window[:].indirect(listed(cols)), COPY)
 
         first_codes = keep.tile([P, N + NQ], U32, name="first_codes", tag="c01_raw", align_bytes=DMA_ALIGN)
         k_codes = first_codes[:, 0:N]
@@ -95,9 +96,10 @@ def tile_attend_quest_f_topk_kernel(tc, qT, kT, cT, offs, out):
         hi_scales = keep.tile([P, NQ], U8, name="hi_scales", align_bytes=64)
         quantize(k_codes, k_scales, k_grouped, slice(0, N))
         quantize(hi_codes, hi_scales, hi, slice(0, NQ))
+        gather_plane(2, c2_raw)
 
-        groups = [(m, quarters[h]) for m, h in [(0, 0), (1, 0), (0, 1), (1, 1), (0, 2), (1, 2), (0, 3), (1, 3)]]
-        stores = {0: quarters[0], 2: quarters[1], 3: halves[0], 6: halves[1], 7: halves[1]}
+        groups = [(m, quarters[h]) for h in range(len(quarters)) for m in range(2)]
+        stores = {0: quarters[0], 3: halves[0], 6: slice(P, N), 7: halves[1]}
         banks = [psum.tile([P, N], F32, name="bank%d" % g) for g in range(len(groups))]
 
         def multiply(g, q_codes, q_scales, codes, scales, start, stop):
@@ -124,23 +126,17 @@ def tile_attend_quest_f_topk_kernel(tc, qT, kT, cT, offs, out):
         for g in range(len(groups)):
             multiply(g, hi_codes, hi_scales, k_codes, k_scales, True, False)
 
-        pieces = [slice(3 * P, 3 * P + P // 2), quarters[2], slice(3 * P + P // 2, N)]
-        last = {h: keep.tile([P, P // 2], BF16, name="last%d" % h) for h in (0, 2)}
-        nc.vector.tensor_copy(c_grouped[:, halves[0], 3], c3_raw[:].indirect(listed(halves[0])))
-        for staged, cols in zip([last[0][:], late_v[:, 1, :], last[2][:]], pieces):
-            nc.scalar.activation(staged, c3_raw[:].indirect(listed(cols)), COPY)
-        nc.vector.tensor_copy(c_grouped[:, pieces[1], 2:4], late_v[:].rearrange("p t n -> p n t"))
-        for h in (0, 2):
-            nc.scalar.activation(c_grouped[:, pieces[h], 3], last[h][:], COPY)
-        c_codes = keep.tile([P, N], U32, name="c_codes", tag="c3_raw", align_bytes=DMA_ALIGN)
+        gather_plane(3, c3_raw)
+        early_codes = keep.tile([P, P], U32, name="early_codes", align_bytes=64)
+        late_codes = keep.tile([P, N], U32, name="late_codes", tag="c3_raw", align_bytes=DMA_ALIGN)
         c_scales = keep.tile([P, N], U8, name="c_scales", align_bytes=64)
         for cols in quarters:
-            quantize(c_codes, c_scales, c_grouped, cols)
+            quantize(late_codes if cols.start else early_codes, c_scales, c_grouped, cols)
 
         result = keep.tile([P, 2, N], F32, name="result", align_bytes=DMA_ALIGN)
         out_rows = out[0].rearrange("(m p) n -> p m n", p=P)
         for g, (m, cols) in enumerate(groups):
-            multiply(g, lo_codes, lo_scales, c_codes, c_scales, False, True)
+            multiply(g, lo_codes, lo_scales, late_codes if cols.start else early_codes, c_scales, False, True)
             if m == 0:
                 nc.scalar.copy(result[:, m, cols], banks[g][:, 0:P])
             else:

@@ -54,7 +54,9 @@ def tile_attend_quest_f_topk_kernel(tc, qT, kT, cT, offs, out):
 
         halves = [slice(0, HALF), slice(HALF, N)]
         quarters = [slice(h * P, (h + 1) * P) for h in range(N // P)]
-        middle = slice(P, 3 * P)
+        middle = slice(3 * P // 2, 7 * P // 2)
+        before = [quarters[0], slice(P, middle.start)]
+        after = slice(middle.stop, N)
         q_tiles = [slice(m * P, (m + 1) * P) for m in range(2)]
 
         q_view = q_raw[:].rearrange("p t w -> p w t")
@@ -84,9 +86,9 @@ def tile_attend_quest_f_topk_kernel(tc, qT, kT, cT, offs, out):
             nc.scalar.activation(c_picked[:, t, :], c01_raw[:, t, :].indirect(listed(halves[1])), COPY)
         nc.scalar.activation(c_grouped[:, halves[1], 0:2], c_picked[:].rearrange("p t n -> p n t"), COPY)
 
-        def gather_plane(t, window):
+        def gather_plane(t, window, pieces):
             nc.vector.tensor_copy(c_grouped[:, middle, t], window[:].indirect(listed(middle)))
-            for cols in (quarters[0], quarters[3]):
+            for cols in pieces:
                 nc.scalar.activation(c_grouped[:, cols, t], window[:].indirect(listed(cols)), COPY)
 
         first_codes = keep.tile([P, N + NQ], U32, name="first_codes", tag="c01_raw", align_bytes=DMA_ALIGN)
@@ -96,7 +98,7 @@ def tile_attend_quest_f_topk_kernel(tc, qT, kT, cT, offs, out):
         hi_scales = keep.tile([P, NQ], U8, name="hi_scales", align_bytes=64)
         quantize(k_codes, k_scales, k_grouped, slice(0, N))
         quantize(hi_codes, hi_scales, hi, slice(0, NQ))
-        gather_plane(2, c2_raw)
+        gather_plane(2, c2_raw, [slice(0, middle.start), after])
 
         groups = [(m, quarters[h]) for h in range(len(quarters)) for m in range(2)]
         stores = {0: quarters[0], 3: halves[0], 6: slice(P, N), 7: halves[1]}
@@ -126,17 +128,17 @@ def tile_attend_quest_f_topk_kernel(tc, qT, kT, cT, offs, out):
         for g in range(len(groups)):
             multiply(g, hi_codes, hi_scales, k_codes, k_scales, True, False)
 
-        gather_plane(3, c3_raw)
-        early_codes = keep.tile([P, P], U32, name="early_codes", align_bytes=64)
+        gather_plane(3, c3_raw, before + [after])
+        early_codes = keep.tile([P, HALF], U32, name="early_codes", align_bytes=64)
         late_codes = keep.tile([P, N], U32, name="late_codes", tag="c3_raw", align_bytes=DMA_ALIGN)
         c_scales = keep.tile([P, N], U8, name="c_scales", align_bytes=64)
         for cols in quarters:
-            quantize(late_codes if cols.start else early_codes, c_scales, c_grouped, cols)
+            quantize(early_codes if cols.start < HALF else late_codes, c_scales, c_grouped, cols)
 
         result = keep.tile([P, 2, N], F32, name="result", align_bytes=DMA_ALIGN)
         out_rows = out[0].rearrange("(m p) n -> p m n", p=P)
         for g, (m, cols) in enumerate(groups):
-            multiply(g, lo_codes, lo_scales, late_codes if cols.start else early_codes, c_scales, False, True)
+            multiply(g, lo_codes, lo_scales, early_codes if cols.start < HALF else late_codes, c_scales, False, True)
             if m == 0:
                 nc.scalar.copy(result[:, m, cols], banks[g][:, 0:P])
             else:

@@ -101,7 +101,7 @@ def tile_attend_quest_f_topk_kernel(tc, qT, kT, cT, offs, out):
         gather_plane(2, c2_raw, [slice(0, middle.start), after])
 
         groups = [(m, quarters[h]) for h in range(len(quarters)) for m in range(2)]
-        stores = {0: quarters[0], 3: halves[0], 6: slice(P, N), 7: halves[1]}
+        stores = {1: quarters[0], 3: quarters[1], 7: halves[1]}
         banks = [psum.tile([P, N], F32, name="bank%d" % g) for g in range(len(groups))]
 
         def multiply(g, q_codes, q_scales, codes, scales, start, stop):
@@ -144,4 +144,4 @@ def tile_attend_quest_f_topk_kernel(tc, qT, kT, cT, offs, out):
             else:
                 nc.vector.tensor_copy(result[:, m, cols], banks[g][:, 0:P])
             if g in stores:
-                nc.sync.dma_start(out=out_rows[:, m, stores[g]], in_=result[:, m, stores[g]])
+                nc.sync.dma_start(out=out_rows[:, :, stores[g]], in_=result[:, :, stores[g]])

@@ -18,6 +18,7 @@ P = 128
 PACK = 4
 HALF = N // 2
 WARM_ROWS = 32
+WARM_WIDTHS = (512, 128, 128)
 DMA_ALIGN = 512
 
 
@@ -91,13 +92,12 @@ def tile_attend_quest_f_topk_kernel(tc, qT, kT, cT, offs, out):
             for cols in pieces:
                 nc.scalar.activation(c_grouped[:, cols, t], window[:].indirect(listed(cols)), COPY)
 
-        first_codes = keep.tile([P, N + NQ], U32, name="first_codes", tag="c01_raw", align_bytes=DMA_ALIGN)
-        k_codes = first_codes[:, 0:N]
-        hi_codes = first_codes[:, N : N + NQ]
+        k_codes = keep.tile([P, N], U32, name="k_codes", tag="c01_raw", align_bytes=DMA_ALIGN)
+        hi_codes = keep.tile([P, NQ], U32, name="hi_codes", align_bytes=64)
         k_scales = keep.tile([P, N], U8, name="k_scales", align_bytes=64)
         hi_scales = keep.tile([P, NQ], U8, name="hi_scales", align_bytes=64)
-        quantize(k_codes, k_scales, k_grouped, slice(0, N))
         quantize(hi_codes, hi_scales, hi, slice(0, NQ))
+        quantize(k_codes, k_scales, k_grouped, slice(0, N))
         gather_plane(2, c2_raw, [slice(0, middle.start), after])
 
         groups = [(m, quarters[h]) for h in range(len(quarters)) for m in range(2)]
@@ -116,15 +116,16 @@ def tile_attend_quest_f_topk_kernel(tc, qT, kT, cT, offs, out):
                 stop=stop,
             )
 
-        nc.tensor.matmul_mx(
-            out=banks[-1][0:WARM_ROWS, :],
-            lhsT=hi_codes[:, 0:WARM_ROWS].bitcast(FP8X4),
-            lhsT_scale=hi_scales[:, 0:WARM_ROWS],
-            rhs=k_codes[:, 0:N].bitcast(FP8X4),
-            rhs_scale=k_scales[:],
-            start=True,
-            stop=True,
-        )
+        for width in WARM_WIDTHS:
+            nc.tensor.matmul_mx(
+                out=banks[-1][0:WARM_ROWS, 0:width],
+                lhsT=hi_codes[:, 0:WARM_ROWS].bitcast(FP8X4),
+                lhsT_scale=hi_scales[:, 0:WARM_ROWS],
+                rhs=k_codes[:, 0:width].bitcast(FP8X4),
+                rhs_scale=k_scales[:, 0:width],
+                start=True,
+                stop=True,
+            )
         for g in range(len(groups)):
             multiply(g, hi_codes, hi_scales, k_codes, k_scales, True, False)
 

@@ -101,7 +101,7 @@ def tile_attend_quest_f_topk_kernel(tc, qT, kT, cT, offs, out):
         gather_plane(2, c2_raw, [slice(0, middle.start), after])
 
         groups = [(m, quarters[h]) for h in range(len(quarters)) for m in range(2)]
-        stores = {1: quarters[0], 3: quarters[1], 7: halves[1]}
+        stores = {0: quarters[0], 3: halves[0], 6: slice(P, N), 7: halves[1]}
         banks = [psum.tile([P, N], F32, name="bank%d" % g) for g in range(len(groups))]
 
         def multiply(g, q_codes, q_scales, codes, scales, start, stop):
@@ -140,9 +140,9 @@ def tile_attend_quest_f_topk_kernel(tc, qT, kT, cT, offs, out):
         out_rows = out[0].rearrange("(m p) n -> p m n", p=P)
         for g, (m, cols) in enumerate(groups):
             multiply(g, lo_codes, lo_scales, early_codes if cols.start < HALF else late_codes, c_scales, False, True)
-            if m == 0:
+            if m == 1:
                 nc.scalar.copy(result[:, m, cols], banks[g][:, 0:P])
             else:
                 nc.vector.tensor_copy(result[:, m, cols], banks[g][:, 0:P])
             if g in stores:
-                nc.sync.dma_start(out=out_rows[:, :, stores[g]], in_=result[:, :, stores[g]])
+                nc.sync.dma_start(out=out_rows[:, m, stores[g]], in_=result[:, m, stores[g]])

@@ -55,9 +55,7 @@ def tile_attend_quest_f_topk_kernel(tc, qT, kT, cT, offs, out):
 
         halves = [slice(0, HALF), slice(HALF, N)]
         quarters = [slice(h * P, (h + 1) * P) for h in range(N // P)]
-        middle = slice(3 * P // 2, 7 * P // 2)
-        before = [quarters[0], slice(P, middle.start)]
-        after = slice(middle.stop, N)
+        first_pieces = [quarters[0], slice(P, 3 * P // 2), slice(3 * P // 2, HALF)]
         q_tiles = [slice(m * P, (m + 1) * P) for m in range(2)]
 
         q_view = q_raw[:].rearrange("p t w -> p w t")
@@ -88,7 +86,7 @@ def tile_attend_quest_f_topk_kernel(tc, qT, kT, cT, offs, out):
         nc.scalar.activation(c_grouped[:, halves[1], 0:2], c_picked[:].rearrange("p t n -> p n t"), COPY)
 
         def gather_plane(t, window, pieces):
-            nc.vector.tensor_copy(c_grouped[:, middle, t], window[:].indirect(listed(middle)))
+            nc.vector.tensor_copy(c_grouped[:, halves[1], t], window[:].indirect(listed(halves[1])))
             for cols in pieces:
                 nc.scalar.activation(c_grouped[:, cols, t], window[:].indirect(listed(cols)), COPY)
 
@@ -98,7 +96,7 @@ def tile_attend_quest_f_topk_kernel(tc, qT, kT, cT, offs, out):
         hi_scales = keep.tile([P, NQ], U8, name="hi_scales", align_bytes=64)
         quantize(hi_codes, hi_scales, hi, slice(0, NQ))
         quantize(k_codes, k_scales, k_grouped, slice(0, N))
-        gather_plane(2, c2_raw, [slice(0, middle.start), after])
+        gather_plane(2, c2_raw, [halves[0]])
 
         groups = [(m, quarters[h]) for h in range(len(quarters)) for m in range(2)]
         stores = {0: quarters[0], 3: halves[0], 6: slice(P, N), 7: halves[1]}
@@ -129,11 +127,11 @@ def tile_attend_quest_f_topk_kernel(tc, qT, kT, cT, offs, out):
         for g in range(len(groups)):
             multiply(g, hi_codes, hi_scales, k_codes, k_scales, True, False)
 
-        gather_plane(3, c3_raw, before + [after])
+        gather_plane(3, c3_raw, first_pieces)
         early_codes = keep.tile([P, HALF], U32, name="early_codes", align_bytes=64)
         late_codes = keep.tile([P, N], U32, name="late_codes", tag="c3_raw", align_bytes=DMA_ALIGN)
         c_scales = keep.tile([P, N], U8, name="c_scales", align_bytes=64)
-        for cols in quarters:
+        for cols in first_pieces + quarters[2:]:
             quantize(early_codes if cols.start < HALF else late_codes, c_scales, c_grouped, cols)
 
         result = keep.tile([P, 2, N], F32, name="result", align_bytes=DMA_ALIGN)

from contextlib import ExitStack

import concourse.mybir as mybir

D, T, N, NQ = 512, 2048, 512, 256
FLOPS = 2 * 2 * NQ * D * N

F32 = mybir.dt.float32
BF16 = mybir.dt.bfloat16
U32 = mybir.dt.uint32
U16 = mybir.dt.uint16
U8 = mybir.dt.uint8
FP8X4 = mybir.dt.float8_e4m3fn_x4
RELU = mybir.ActivationFunctionType.Relu
COPY = mybir.ActivationFunctionType.Copy

P = 128
PACK = 4
HALF = N // 2
WARM_ROWS = 32
WARM_WIDTHS = (512, 128, 128)
DMA_ALIGN = 512


def tile_attend_quest_f_topk_kernel(tc, qT, kT, cT, offs, out):
    nc = tc.nc
    with ExitStack() as ctx:
        keep = ctx.enter_context(tc.tile_pool(name="keep", bufs=1))
        psum = ctx.enter_context(tc.psum_pool(name="psum", bufs=1))

        offsets = keep.tile([P, N // 16], U16, name="offsets")
        q_raw = keep.tile([P, PACK, NQ], F32, name="q_raw", align_bytes=DMA_ALIGN)
        k_raw = keep.tile([P, PACK, T], F32, name="k_raw", align_bytes=DMA_ALIGN)
        c01_raw = keep.tile([P, 2, T], F32, name="c01_raw", tag="c01_raw", align_bytes=DMA_ALIGN)
        c2_raw = keep.tile([P, T], F32, name="c2_raw", align_bytes=DMA_ALIGN)
        c3_raw = keep.tile([P, T], F32, name="c3_raw", tag="c3_raw", align_bytes=DMA_ALIGN)
        c_rows = cT.rearrange("(p t) w -> p t w", t=PACK)

        nc.scalar.dma_start(out=q_raw[:], in_=qT[0].rearrange("(p t) w -> p t w", t=PACK))
        nc.sync.dma_start(offsets[:], offs)
        nc.sync.dma_start(out=k_raw[:], in_=kT.rearrange("(p t) w -> p t w", t=PACK))
        nc.sync.dma_start(out=c01_raw[:], in_=c_rows[:, 0:2, :])
        nc.sync.dma_start(out=c2_raw[:], in_=c_rows[:, 2, :])
        nc.sync.dma_start(out=c3_raw[:], in_=c_rows[:, 3, :])

        def quantize(codes, scales, grouped, cols):
            nc.vector.quantize_mx(
                out=codes[:, cols].bitcast(FP8X4),
                scales=scales[:, cols],
                in_=grouped[:, cols, :].rearrange("p w t -> p (w t)"),
            )

        def listed(cols):
            return offsets[:, cols.start // 16 : cols.stop // 16]

        halves = [slice(0, HALF), slice(HALF, N)]
        quarters = [slice(h * P, (h + 1) * P) for h in range(N // P)]
        first_pieces = [quarters[0], slice(P, 3 * P // 2), slice(3 * P // 2, HALF)]
        q_tiles = [slice(m * P, (m + 1) * P) for m in range(2)]

        q_view = q_raw[:].rearrange("p t w -> p w t")
        hi = keep.tile([P, NQ, PACK], BF16, name="hi", align_bytes=64)
        lo = keep.tile([P, NQ, PACK], BF16, name="lo", align_bytes=64)
        nc.scalar.activation(hi[:], q_view, RELU)
        nc.vector.tensor_scalar_min(lo[:], q_view, 0.0)
        lo_codes = keep.tile([P, NQ], U32, name="lo_codes", align_bytes=64)
        lo_scales = keep.tile([P, NQ], U8, name="lo_scales", align_bytes=64)
        quantize(lo_codes, lo_scales, lo, slice(0, NQ))

        k_grouped = keep.tile([P, N, PACK], BF16, name="k_grouped", align_bytes=64)
        c_grouped = keep.tile([P, N, PACK], BF16, name="c_grouped", align_bytes=64)
        k_picked = keep.tile([P, PACK, HALF], F32, name="k_picked")
        for t in range(PACK):
            nc.vector.tensor_copy(k_grouped[:, halves[0], t], k_raw[:, t, :].indirect(listed(halves[0])))
            nc.scalar.activation(k_picked[:, t, :], k_raw[:, t, :].indirect(listed(halves[1])), COPY)
        nc.scalar.activation(
            k_grouped[:, halves[1], :].rearrange("p (c i) t -> p c t i", i=4),
            k_picked[:].rearrange("p t (c i) -> p c t i", i=4),
            COPY,
        )

        c_picked = keep.tile([P, 2, HALF], F32, name="c_picked")
        for t in range(2):
            nc.vector.tensor_copy(c_grouped[:, halves[0], t], c01_raw[:, t, :].indirect(listed(halves[0])))
            nc.scalar.activation(c_picked[:, t, :], c01_raw[:, t, :].indirect(listed(halves[1])), COPY)
        nc.scalar.activation(c_grouped[:, halves[1], 0:2], c_picked[:].rearrange("p t n -> p n t"), COPY)

        def gather_plane(t, window, pieces):
            nc.vector.tensor_copy(c_grouped[:, halves[1], t], window[:].indirect(listed(halves[1])))
            for cols in pieces:
                nc.scalar.activation(c_grouped[:, cols, t], window[:].indirect(listed(cols)), COPY)

        k_codes = keep.tile([P, N], U32, name="k_codes", tag="c01_raw", align_bytes=DMA_ALIGN)
        hi_codes = keep.tile([P, NQ], U32, name="hi_codes", align_bytes=64)
        k_scales = keep.tile([P, N], U8, name="k_scales", align_bytes=64)
        hi_scales = keep.tile([P, NQ], U8, name="hi_scales", align_bytes=64)
        quantize(hi_codes, hi_scales, hi, slice(0, NQ))
        quantize(k_codes, k_scales, k_grouped, slice(0, N))
        gather_plane(2, c2_raw, [halves[0]])

        groups = [(m, quarters[h]) for h in range(len(quarters)) for m in range(2)]
        stores = {0: quarters[0], 3: halves[0], 6: slice(P, N), 7: halves[1]}
        banks = [psum.tile([P, N], F32, name="bank%d" % g) for g in range(len(groups))]

        def multiply(g, q_codes, q_scales, codes, scales, start, stop):
            m, cols = groups[g]
            nc.tensor.matmul_mx(
                out=banks[g][:, 0:P],
                lhsT=q_codes[:, q_tiles[m]].bitcast(FP8X4),
                lhsT_scale=q_scales[:, q_tiles[m]],
                rhs=codes[:, cols].bitcast(FP8X4),
                rhs_scale=scales[:, cols],
                start=start,
                stop=stop,
            )

        for width in WARM_WIDTHS:
            nc.tensor.matmul_mx(
                out=banks[-1][0:WARM_ROWS, 0:width],
                lhsT=hi_codes[:, 0:WARM_ROWS].bitcast(FP8X4),
                lhsT_scale=hi_scales[:, 0:WARM_ROWS],
                rhs=k_codes[:, 0:width].bitcast(FP8X4),
                rhs_scale=k_scales[:, 0:width],
                start=True,
                stop=True,
            )
        for g in range(len(groups)):
            multiply(g, hi_codes, hi_scales, k_codes, k_scales, True, False)

        gather_plane(3, c3_raw, first_pieces)
        early_codes = keep.tile([P, HALF], U32, name="early_codes", align_bytes=64)
        late_codes = keep.tile([P, N], U32, name="late_codes", tag="c3_raw", align_bytes=DMA_ALIGN)
        c_scales = keep.tile([P, N], U8, name="c_scales", align_bytes=64)
        for cols in first_pieces + quarters[2:]:
            quantize(early_codes if cols.start < HALF else late_codes, c_scales, c_grouped, cols)

        result = keep.tile([P, 2, N], F32, name="result", align_bytes=DMA_ALIGN)
        out_rows = out[0].rearrange("(m p) n -> p m n", p=P)
        for g, (m, cols) in enumerate(groups):
            multiply(g, lo_codes, lo_scales, early_codes if cols.start < HALF else late_codes, c_scales, False, True)
            if m == 1:
                nc.scalar.copy(result[:, m, cols], banks[g][:, 0:P])
            else:
                nc.vector.tensor_copy(result[:, m, cols], banks[g][:, 0:P])
            if g in stores:
                nc.sync.dma_start(out=out_rows[:, m, stores[g]], in_=result[:, m, stores[g]])
